import numpy as np, ml_dtypes
CORES = [2,6,10,14,18,22,26,30]
N = 8
BF = ml_dtypes.bfloat16
def gentries(a):
    return np.ascontiguousarray(a.reshape(8, 16, -1).transpose(0, 2, 1)).reshape(8, -1)
def gtable(e):
    e = np.asarray(e); return np.ascontiguousarray(e.reshape(8, -1, 16).transpose(0, 2, 1)).reshape(128, -1).astype(np.int32)
V, E, G, P, K, J, RO, CM = 1024, 2048, 128, 2944, 8, 6, 3, 63
NEED = 9
NV = (9, 8, 16, 15, 0, 9, 8, 7)
NI = 2 * (K - 1) + 2 * (N - 1) * K
def cover(rng):
    return ((CM + 1) * (0.5 * rng.random((1, V)) + 0.5 * rng.random((16, V)))).astype(np.int64)
def blank():
    return np.full((K, E), -1), np.ones((K, P), bool)
def put(L, free, i, e, t):
    if L[i, e] < 0 and free[i, t]:
        L[i, e] = t; free[i, t] = False
def pair(L, free, c, l, e, f, up=0, down=0):
    i = (c[e] + l) % K; j = (c[f] + l) % K
    ok = (L[i, e] < 0) & (L[j, f] < 0) & free[i, f + up] & free[j, e + down]
    i, j, e, f = i[ok], j[ok], e[ok], f[ok]
    L[i, e] = f + up; L[j, f] = e + down; free[i, f + up] = False; free[j, e + down] = False
def sides(rng, reads):
    s = rng.integers(0, 2, len(reads)); return 2 * reads + s, 2 * reads + 1 - s
def weave(rng, L, free, c, reads, q):
    a, b = sides(rng, reads); b = np.roll(b, -1); keep = rng.random(len(reads)) >= q; more = keep & (rng.random(len(reads)) < 0.33)
    pair(L, free, c, 0, a[keep], b[keep]); pair(L, free, c, 1, a[more], b[more])
    u = np.concatenate([a[~keep], b[~keep]])
    v = rng.permutation(u[(u < (N - 1) * G) & (u % G < G - 8)])[:8]; k = len(v) // 4
    pair(L, free, c, 0, v[:k], v[k:2 * k], E, E); pair(L, free, c, 0, v[2 * k:3 * k], v[3 * k:4 * k], E, 0)
    for l in range(1, RO):
        u = rng.permutation(u); k = 3 * len(u) // 10; pair(L, free, c, l, u[:k], u[k:2 * k]); u = u[2 * k:]
def fill(rng, L, free, shut):
    free[:, shut] = False
    for i in range(K):
        e = np.flatnonzero(L[i] < 0); L[i, e] = rng.permutation(np.flatnonzero(free[i]))[:len(e)]
def closed(reads, k):
    reads = np.asarray(reads, np.int64)
    return np.concatenate([2 * reads, 2 * reads + 1] + [E + d * G + G - 1 - np.arange(k) for d in range(N - 1)]).astype(np.int64)
def show(rng, pool, last):
    return np.concatenate([rng.permutation(pool)[:G - len(last)], np.array(last, np.int64)])
def join(rng, L, free, c, reads, k):
    s = rng.integers(0, 2, len(reads)); s[k - 1] = reads[k - 1] & 1
    o, n = 2 * reads + s, 2 * reads + 1 - s; pair(L, free, c, 0, o[:-1], n[1:]); return o, n
def duel(rng, L, free, c, X, Y, Z, t, s):
    o, n = join(rng, L, free, c, np.concatenate([X, Y]), len(X)); f, b = int(o[len(X) - 1]), int(n[len(X)])
    o, n = join(rng, L, free, c, Z, len(Z)); e, h = int(o[-1]), int(n[0])
    if (c[e] + t - c[b]) % K == 0: c[e] = K - 1 - c[e]
    for l in range(t, RO): put(L, free, (c[e] + l) % K, e, f)
    for l in range(s, RO): put(L, free, (c[h] + l) % K, h, E + ((N - 2 + l - s) % (N - 1)) * G + G - 1)
    return f, e
def paint(rng, x, X, Y, Z, nv, inv, near):
    hi, lo = (0, CM) if inv else (CM, 0); on = rng.permutation(16)[:nv]
    x[:, X] = hi; x[:, Y] = lo; x[:, Z] = lo
    if near: x[on, Z[-1]] = CM - 1 if inv else 1
    else: x[np.ix_(on, Z)] = hi
def edge(me, mf, mh, d):
    wf = next(w for w in range(CM * mf // 2, 0, -1) if (2 * w * mh * me - d) % mf == 0); s = (2 * wf * mh * me - d) // mf
    we = next(w for w in range(s // mh, 0, -1) if (s - w * mh) % me == 0)
    return we, wf, (s - we * mh) // me
def fine(rng, L, free, c, x, X, Y, Z, t, nv, inv):
    duel(rng, L, free, c, X, Y, Z, t, RO)
    p = np.concatenate([rng.permutation(np.array([0, 1, 14, 15])), 2 + rng.permutation(12)])
    if nv < NEED: p = p[::-1]
    for j in range(16):
        for q, s in zip((Z, X, Y), edge(len(Z), len(X), len(Y), 1 if j < nv else -(j % 2))):
            v = s // len(q) + (np.arange(len(q)) < s % len(q)); x[p[j], q] = CM - v if inv else v
def draw(rng, one):
    t = [[one(rng, r, g) for g in range(8)] for r in range(N)]
    x, c, L, s = [np.stack([np.stack([a[i] for a in row]) for row in t]) for i in range(4)]
    return {"cov": np.ascontiguousarray(x.reshape(N, 128, V)).astype(np.float32).astype(BF), "cand": np.stack([gtable(a.reshape(8, -1)) for a in L]),
            "shown": np.stack([gtable(a) for a in s]), "cur0": np.stack([gtable(a) for a in c])}
def plain(rng, r, g):
    c = rng.integers(0, K, E); L, free = blank()
    weave(rng, L, free, c, rng.permutation(V), rng.choice(np.array([0.01, 0.05, 0.15, 0.3, 0.5]))); fill(rng, L, free, closed([], 0))
    return cover(rng), c, L, show(rng, np.arange(E), [])
def uneven(rng, r, g):
    c = np.minimum((K * rng.random(E) ** rng.choice(np.array([0.25, 1.0, 4.0]))).astype(np.int64), K - 1); L, free = blank()
    weave(rng, L, free, c, rng.permutation(V), rng.choice(np.array([0.02, 0.1, 0.4, 0.8]))); fill(rng, L, free, closed([], 0))
    x = np.exp2(np.log2(CM + 1.0) * rng.random((1, V))) * rng.random((16, V)) ** rng.choice(np.array([0.25, 1.0, 3.0]), (16, 1))
    return np.minimum(x.astype(np.int64), CM), c, L, show(rng, np.arange(E), [])
def atends(rng, r, g):
    n = 2 ** J; m = G // 4; c = (K - 1) * rng.integers(0, 2, E); L, free = blank()
    lx, ly, lz = [n + (int(rng.choice(np.array([0, 0, 1, -1, -3]))) if g < 6 else 0) for i in range(3)]
    a, z = (V - 1, 0) if (r + g) % 2 == 0 else (0, V - 1)
    mid = rng.permutation(np.arange(m, V - m)); k = lx - 1 + ly
    X = np.append(mid[:lx - 1], a); Y = mid[lx - 1:k]; Z = np.append(mid[k:k + lz - 1], z); mid = mid[k + lz - 1:]
    f, e = duel(rng, L, free, c, X, Y, Z, (r + g) % RO, (r + 2 * g) % RO)
    weave(rng, L, free, c, rng.permutation(np.concatenate([mid, np.arange(1, m), np.arange(V - m, V - 1)])), rng.choice(np.array([0.05, 0.2, 0.4])))
    fill(rng, L, free, closed(np.concatenate([X, Y, Z]), 3))
    x = CM * (rng.random((16, V)) < rng.choice(np.array([0.0, 0.1, 0.5, 1.0]), (1, V))).astype(np.int64)
    paint(rng, x, X, Y, Z, NV[(5 * (N - 1 - r) + 7 - g) % 8], g % 2 == 0, False)
    last = [e ^ 1, f ^ 1, f]
    return x, c, L, show(rng, np.setdiff1d(np.concatenate([np.arange(2 * m), np.arange(E - 2 * m, E)]), last), last)
def corner(rng, r, g, role):
    n = 2 ** J; c = np.full(E, (0, 1, 2, 3, K - 1, K - 2)[(r + role) % 6] % K); L, free = blank(); o = rng.permutation(V)
    x = cover(rng); x[:, 0::5] = 0; x[:, 1::5] = CM; pool = np.arange(E); last = []; shut = closed([], 0)
    if role < 2: weave(rng, L, free, c, o, float((r + role) % 2))
    elif role == 2:
        h = V // 2; k = h + h // 2; pair(L, free, c, 0, 2 * o[:h], 2 * o[:h] + 1)
        u = np.concatenate([2 * o[h:k], 2 * o[h:k] + 1])
        for e in u: put(L, free, c[e], e, e)
        u = rng.permutation(u); w = len(u) // 4; pair(L, free, c, 1, u[:w], u[w:2 * w]); weave(rng, L, free, c, o[k:], 0.3)
    elif role == 3:
        k = 0; i = r
        while k < V:
            w = min((1, 2, n - 1, n, n + 1, 3, 2 * n)[i % 7], V - k); a, b = sides(rng, o[k:k + w]); pair(L, free, c, 0, a[:-1], b[1:])
            if rng.random() < 0.4: pair(L, free, c, 0, a[-1:], b[:1])
            k += w; i += 1
        u = rng.permutation(np.flatnonzero(L[c, np.arange(E)] < 0)); w = 3 * len(u) // 10; pair(L, free, c, 1, u[:w], u[w:2 * w])
    else:
        lx, ly, lz = [int(v) for v in rng.choice(np.array([1, 2, n - 1, n, n + 1]), 3)]; k = lx + ly + lz
        X, Y, Z = o[:lx], o[lx:lx + ly], o[lx + ly:k]
        f, e = duel(rng, L, free, c, X, Y, Z, (r + role) % RO, (r + g) % RO); weave(rng, L, free, c, o[k:], 0.3)
        paint(rng, x, X, Y, Z, NV[(3 * r + role) % 8], r % 2 == 1 and role < 6, role % 2 == 1)
        last = [f]; pool = np.concatenate([2 * o[k:], 2 * o[k:] + 1]); shut = closed(o[:k], 1)
    fill(rng, L, free, shut)
    return x, c, L, show(rng, pool, last)
def ballots(rng):
    a, b = K - 1, 2 * (K - 1); v = np.full((N, 8, 4, NI), 8); s = b + K * np.arange(2 * (N - 1))
    first = np.unique(np.concatenate([np.array([0, a - 1, a, b - 1]), s, s + K - 1]))
    one = np.concatenate([rng.permutation(first), rng.permutation(np.setdiff1d(np.arange(NI), first))]); u = rng.permutation(8 * N).reshape(N, 8)
    top = 16
    while 2 * top <= NI: top = 2 * top
    for q in range(N):
        for g in range(8):
            for h in range(4):
                kind = (g + h) % 4; o = rng.permutation(NI)
                if kind == 0: v[q, g, h, o[q % 2:]] = 16
                elif kind == 1: v[q, g, h, one[u[q, g] % NI]] = 9
                elif kind == 3:
                    w = (16, top)[q % 2]; v[q, g, h, o[:w]] = 15 + rng.integers(0, 2, w)
    return v
def crowd(rng, r, g, votes):
    n = 2 ** J; c = rng.integers(0, K, E); L, free = blank(); x = cover(rng); o = rng.permutation(V); k = 0; hubs = []
    for h in range(4):
        lx, ly = [int(v) for v in rng.integers(1, 6, 2)]; xy = o[k:k + lx + ly]; k += lx + ly
        a, b = join(rng, L, free, c, xy, lx); hubs.append((int(a[lx - 1]), int(b[lx]))); x[:, xy[:lx]] = CM; x[:, xy[lx:]] = 0
    lx, ly, lz = ((n - 1, n, n - 3), (n - 1, n - 3, n), (n - 3, n, n - 1), (n - 3, n - 1, n))[(r + g // 2) % 4]; w = o[k:k + lx + ly + lz]; k += len(w)
    fine(rng, L, free, c, x, w[:lx], w[lx:lx + ly], w[lx + ly:], (r + 2 * g) % RO, (9, 8)[(r + g) % 2], rng.random() < 0.5)
    shut = closed(o[:k], 8)
    for h, (f, b) in enumerate(hubs):
        t = h % RO; on = rng.permutation(16); mine = votes[r, g, h]
        jobs = [(i, f, CM, mine[j]) for j, i in enumerate([y for y in range(K) if y != c[b]])]
        jobs += [(i, b, 0, mine[K - 1 + j]) for j, i in enumerate([y for y in range(K) if y != c[f]])]
        jobs += [(i, E + d * G + G - 1 - h - 4 * s, CM * (1 - s), votes[(r - d - 1) % N, (g + 2) % 8, h, 2 * (K - 1) + (s * (N - 1) + d) * K + i]) for s in range(2) for d in range(N - 1) for i in range(K)]
        for j, (i, p, v, nv) in enumerate(jobs):
            z = int(o[k]); k += 1; e = 2 * z + (j + h) % 2; c[e] = (i - t) % K; put(L, free, i, e, p)
            x[:, z] = CM - v; x[on[:nv], z] = v
    weave(rng, L, free, c, o[k:], rng.choice(np.array([0.05, 0.2, 0.4]))); fill(rng, L, free, shut)
    return x, c, L, show(rng, np.concatenate([2 * o[k:], 2 * o[k:] + 1]), [b for f, b in hubs[::-1]] + [f for f, b in hubs[::-1]])
def setup_inputs(rng):
    return draw(rng, plain)
def setup_inputs_spread(rng):
    return draw(rng, uneven)
def setup_inputs_ends(rng):
    return draw(rng, atends)
def setup_inputs_corners(rng):
    role = np.zeros(8, np.int64); p = int(rng.integers(0, 2)); role[p::2] = 4 + rng.permutation(4); role[1 - p::2] = rng.permutation(4)
    return draw(rng, lambda rng, r, g: corner(rng, r, g, int(role[g])))
def setup_inputs_crowd(rng):
    votes = ballots(rng)
    return draw(rng, lambda rng, r, g: crowd(rng, r, g, votes))
def check_inputs(d):
    bad = []
    x = np.asarray(d["cov"]).astype(np.float64)
    if not (np.all(x >= 0) and np.all(x <= CM) and np.all(x == np.floor(x))): bad.append("range of cov")
    for k, hi in (("cand", P - 1), ("shown", E - 1), ("cur0", K - 1)):
        if np.min(d[k]) < 0 or np.max(d[k]) > hi: bad.append("range of " + k)
    for k, m in (("cand", E), ("shown", G)):
        a = np.sort(np.stack([gentries(t) for t in d[k]]).reshape(N, 8, -1, m), axis=-1)
        if np.any(a[..., 1:] == a[..., :-1]): bad.append("a number twice in " + k)
    return bad
def seen(a, sl):
    s = np.take_along_axis(a, sl if a.ndim == 3 else sl[:, :, None, :], -1)
    return np.stack([np.concatenate([a[r]] + [np.roll(s[(r - d) % N], -2, axis=0) for d in range(1, N)], axis=-1) for r in range(N)])
def reference(cov, cand, shown, cur0):
    pick = np.take_along_axis; ar = np.arange(E)
    x = np.repeat(cov.astype(np.float32).astype(np.int32).reshape(N, 8, 16, V), 2, axis=3)
    x = np.concatenate([x, np.zeros((N, 8, 16, 1), np.int32)], axis=3)
    cl = np.stack([gentries(a) for a in cand]).astype(np.int64).reshape(N, 8, K, E)
    sl = np.stack([gentries(a) for a in shown]).astype(np.int64); c = np.stack([gentries(a) for a in cur0]).astype(np.int64)
    for rnd in range(RO):
        b = pick(cl, c[:, :, None, :], 2)[:, :, 0]
        own = b < E
        link = own & (b != ar) & (pick(b, np.where(own, b, ar), 2) == ar)
        nx = np.concatenate([np.where(link, b ^ 1, E), np.full((N, 8, 1), E)], axis=2)
        S = x; n = np.concatenate([np.ones((N, 8, E), np.int32), np.zeros((N, 8, 1), np.int32)], axis=2)
        for j in range(J):
            S = S + pick(S, nx[:, :, None, :], 3); n = n + pick(n, nx, 2); nx = pick(nx, nx, 2)
        w = S[..., ar ^ 1]; m = n[..., ar ^ 1]; pt = np.where(link, b, ar)
        wp = pick(w, pt[:, :, None, :], 3); mp = pick(m, pt, 2)
        bw = b[:, :, None, :]
        wf = pick(seen(w, sl), bw, 3); wh = pick(seen(wp, sl), bw, 3)
        mf = pick(seen(m, sl), b, 2)[:, :, None, :]; mh = pick(seen(mp, sl), b, 2)[:, :, None, :]; lf = pick(seen(link, sl), b, 2)
        m1 = m[:, :, None, :]
        vote = np.abs(w * mf - wf * m1) * mh < np.abs(wh * mf - wf * mh) * m1
        cut = ~link & lf & (np.add.reduce(vote.astype(np.int32), axis=2) >= NEED)
        hit = np.zeros((N, 8, P), bool)
        for r in range(N):
            for g in range(8): hit[r, g, b[r, g][cut[r, g]]] = True
        gone = np.array(hit[:, :, :E])
        for q in range(N):
            for d in range(1, N):
                for g in range(8): gone[q, g, sl[q, g][hit[(q + d) % N, (g - 2) % 8, E + (d - 1) * G:E + d * G]]] = True
        gone = gone | pick(gone, pt, 2)
        c = (c + (~link | gone).astype(np.int64)) % K
    return {"yc": np.stack([gtable(a) for a in c]).astype(np.float32), "ys": np.ascontiguousarray(S[..., :E]).reshape(N, 128, E).astype(np.float32)}

@@ -1,0 +1,642 @@
+from concourse.bass import DstId, RemoteDMATransfer
+from concourse.mybir import AluOpType as ALU, ActivationFunctionType as AF
+
+E, NP, NR, HG = 2048, 2944, 8, 2064
+GB, MO, MF, AO, WE = 2048, 4736, 6784, 7680, 9728
+MAGIC = 1.5 * 2.0 ** 35
+F, B, I, U = "float32", "bfloat16", "int32", "uint16"
+SCRATCH = {
+    "WIN": ("sbuf", [128, WE], F), "X0": ("sbuf", [128, 2064], F), "UA": ("sbuf", [128, 2064], F),
+    "UB": ("sbuf", [128, 2064], F), "MH": ("sbuf", [128, 2048], F), "A1": ("sbuf", [128, 2048], F),
+    "X1": ("sbuf", [128, 2048], F), "H2": ("sbuf", [128, 2048], B), "XS": ("sbuf", [128, 8 * NP], B), "H": ("sbuf", [128, HG + 896], B), "TT": ("sbuf", [128, 2064], B),
+    "WN": ("sbuf", [128, 2176], B), "WP": ("sbuf", [128, 2176], B), "NA": ("sbuf", [128, 2064], B), "NB": ("sbuf", [128, 2064], B),
+    "EX": ("sbuf", [128, 2048], B), "XH": ("sbuf", [128, 2048], B), "XL": ("sbuf", [128, 2048], B),
+    "CV": ("sbuf", [128, 1024], B), "CD": ("sbuf", [128, 1024], I), "CI": ("sbuf", [128, 128], I), "SI": ("sbuf", [128, 8], I),
+    "OF": ("sbuf", [128, 16 * 128], U), "OP": ("sbuf", [128, 64], U),
+    "W": ("sbuf", [128, 32 * 128], F), "WI": ("sbuf", [128, 5 * 128], I), "HL": ("sbuf", [128, 256], B), "BL": ("sbuf", [128, 768], B),
+    "K": ("sbuf", [128, 5 * 128], F), "KB": ("sbuf", [128, 8 * 128], B), "PC": ("sbuf", [128, 8], F), "PI": ("sbuf", [128, 8], I),
+    "PG": ("sbuf", [128, 512], F), "PAY": ("sbuf", [128, 384], F), "PF": ("sbuf", [128, 384], F), "SG": ("sbuf", [128, 768], B),
+    "RET": ("sbuf", [128, 896], B), "RV": ("sbuf", [128, 512], B), "SM": ("sbuf", [128, 64], F),
+    "PM": ("psum", [128, 2048], F), "PA": ("psum", [128, 512], F), "PB": ("psum", [128, 512], F),
+    "PX": ("psum", [128, 512], F), "PY": ("psum", [128, 512], F),
+}
+SEMAPHORES = ["cv", "cs", "ct", "cg", "ld0", "ld1", "ld2", "ld3", "ld4", "xz", "dg", "do", "oy", "oc", "sent", "fwd", "rsent", "ret"] + \
+             ["ga%d" % d for d in range(1, 8)]
+
+
+def rank_program(g, core, T, topo):
+    rank = T.rank_of(core)
+    if rank is None:
+        return
+    cores = list(T.cores)
+    Q = {"v": g.vector, "s": g.scalar, "t": g.tensor, "g": g, "y": g.sync}
+    ops, acc, cnt = [], {}, {}
+
+    def r(name, lo=None, hi=None, step=None, p=None):
+        w = SCRATCH[name][1][1]
+        lo = 0 if lo is None else lo
+        hi = w if hi is None else hi
+        ps = slice(None) if p is None else p
+        ap = T[name][ps, lo:hi] if step is None else T[name][ps, lo:hi:step]
+        return {"ap": ap, "rg": [(name, lo, hi)], "off": []}
+
+    def ind(win, off):
+        return {"ap": win["ap"].indirect(off["ap"]), "rg": win["rg"], "off": off["rg"]}
+
+    def add(q, fn, wr, rd, kind="c", sem=None, inc=0, after=()):
+        k = len(ops)
+        W_ = [x for a in wr for x in a["rg"]]
+        R_ = [x for a in rd for x in a["rg"]] + [x for a in list(wr) + list(rd) for x in a["off"]]
+        deps = set(after)
+        for rg, isw in [(x, True) for x in W_] + [(x, False) for x in R_]:
+            ps = SCRATCH[rg[0]][0] == "psum"
+            for (j, lo, hi, jw) in acc.get(rg[0], []):
+                o = ops[j]
+                if ps and o["q"] != q:
+                    if lo // 512 <= (rg[2] - 1) // 512 and rg[1] // 512 <= (hi - 1) // 512:
+                        deps.add(j)
+                    continue
+                if hi <= rg[1] or rg[2] <= lo or not (jw or isw) or (q == "t" and o["q"] == "t"):
+                    continue
+                if not (kind == "d" and o["kind"] == "d" and o["sem"] == sem):
+                    deps.add(j)
+        for rg, isw in [(x, True) for x in W_] + [(x, False) for x in R_]:
+            acc.setdefault(rg[0], []).append((k, rg[1], rg[2], isw))
+        waits = {}
+        for j in deps:
+            o = ops[j]
+            if o["kind"] != "c":
+                waits[o["sem"]] = cnt[o["sem"]]
+        if sem is not None:
+            cnt[sem] = cnt.get(sem, 0) + inc
+        ops.append({"q": q, "fn": fn, "kind": kind, "sem": sem, "deps": sorted(deps), "waits": waits, "tot": cnt.get(sem, 0)})
+        return k
+
+    def tc(out, a, q="v"):
+        if q == "s":
+            return act(out, a, AF.Identity)
+        return add("v", lambda: g.vector.tensor_copy(out["ap"], a["ap"]), [out], [a])
+
+    def tt(out, a, b, op):
+        return add("v", lambda: g.vector.tensor_tensor(out["ap"], a["ap"], b["ap"], op), [out], [a, b])
+
+    def ts(out, a, s1, op0, s2=None, op1=None):
+        rd = [a] + [x for x in (s1, s2) if isinstance(x, dict)]
+        v1 = s1["ap"] if isinstance(s1, dict) else s1
+        v2 = s2["ap"] if isinstance(s2, dict) else s2
+        if op1 is None:
+            return add("v", lambda: g.vector.tensor_scalar(out["ap"], a["ap"], v1, None, op0), [out], rd)
+        return add("v", lambda: g.vector.tensor_scalar(out["ap"], a["ap"], v1, v2, op0, op1), [out], rd)
+
+    def ms(out, c):
+        return add("v", lambda: g.vector.memset(out["ap"], c), [out], [])
+
+    def act(out, a, f, scale=1.0, bias=0.0):
+        rd = [a] + ([bias] if isinstance(bias, dict) else [])
+        bv = bias["ap"] if isinstance(bias, dict) else bias
+        return add("s", lambda: g.scalar.activation(out["ap"], a["ap"], f, bias=bv, scale=scale), [out], rd)
+
+    def mm(out, l, x, start, stop):
+        return add("t", lambda: g.tensor.matmul(out["ap"], l["ap"], x["ap"], start, stop), [out], [l, x])
+
+    def mms(out, pairs):
+        for k, (l, x) in enumerate(pairs):
+            mm(out, l, x, k == 0, k == len(pairs) - 1)
+
+    def iota(out, pat, base, ch):
+        return add("g", lambda: g.iota(out["ap"], pat, base, ch, allow_small_or_imprecise_dtypes=True), [out], [])
+
+    def hb(ap):
+        return {"ap": ap, "rg": [], "off": []}
+
+    def dma(q, out, a, sem, after=()):
+        return add(q, lambda: Q[q].dma_start(out["ap"], a["ap"]).then_inc(T.sem[sem], 16), [out], [a], "d", sem, 16, after)
+
+    def arrive(sem, n, region):
+        return add("x", None, [region], [], "x", sem, n)
+
+    def send(items, lsem, after=()):
+        trs = []
+        for (dc, src, dst, rs, es) in items:
+            rid, pid, _ = topo.addr(dc)
+            trs.append(RemoteDMATransfer(dst_ids=[DstId(rid=rid, pnc=pid)], dma_engine_mask=sum(1 << e for e in es),
+                                         remote_sem=T.sem[rs], src=src["ap"], dst=dst["ap"]))
+        n = sum(len(it[4]) for it in items)
+        return add("g", lambda: g.remote_dma_fused(trs, local_sem=T.sem[lsem]), [], [it[1] for it in items], "d", lsem, n, after)
+
+    def w(k, n=1):
+        return r("W", k * 128, (k + n) * 128)
+
+    def wh(k, h):
+        return r("W", k * 128 + h * 64, k * 128 + h * 64 + 64)
+
+    def wi(k):
+        return r("WI", k * 128, (k + 1) * 128)
+
+    def of(k, lo=0, hi=128):
+        return r("OF", k * 128 + lo, k * 128 + hi)
+
+    def kf(k):
+        return r("K", k * 128, (k + 1) * 128)
+
+    def kb(k):
+        return r("KB", k * 128, (k + 1) * 128)
+
+    def bl(k):
+        return r("BL", k * 128, (k + 1) * 128)
+
+    def hl(h):
+        return r("HL", h * 128, (h + 1) * 128)
+
+    def ext(src, c0, n, out, more=()):
+        mms(out, list(more) + [(r("EX", i * 128, (i + 1) * 128), r(src, c0 + i, c0 + 16 * n, 16)) for i in range(16)])
+
+    def expand(hi, lo, win, banks):
+        for k in range(4):
+            nm, c0 = banks[k]
+            for i in range(4 * k, 4 * k + 4):
+                mms(r(nm, c0 + (i % 4) * 128, c0 + (i % 4 + 1) * 128),
+                    [(r("XH", i * 128, (i + 1) * 128), hi), (r("XL", i * 128, (i + 1) * 128), lo)])
+        for k in range(4):
+            tc(r(win, k * 512, (k + 1) * 512), r(banks[k][0], banks[k][1], banks[k][1] + 512), "s")
+
+    PMB = [("PM", k * 512) for k in range(4)]
+    ALT = [("PM", 1536), ("PA", 0), ("PB", 0), ("PY", 0)]
+    (cB, cR1, cR2, cBP, cUH, cIO, cEC, cD, cP0, cPU, cDB, t0, t1, t2, t3, t4, t5, t6, t7, cBX, cDX) = range(21)
+    cDD, cE1, cE2, cB0, cDL = 22, 24, 26, 28, 30
+    oN = [0, 2, 3, 4, 5, 6]
+    o1, oBX, oT2, oBU, oBM, oH, oR, oX, oPT = 1, 7, 8, 9, 10, 11, 12, 13, 14
+
+    mate = [q for q in range(NR) if q != rank and topo.chip(cores[q]) == topo.chip(core)]
+    far = [q for q in range(NR) if topo.chip(cores[q]) != topo.chip(core)]
+
+    def gate(a, q):
+        on = [x for x in range(NR) if topo.chip(cores[x]) == topo.chip(cores[q])]
+        same = [x for x in on if topo.die(cores[x]) == topo.die(cores[a])]
+        return (same or on)[0]
+
+    def near(q):
+        return topo.mates(topo.chip(core), topo.chip(cores[q]))
+    direct = sorted([q for q in far if gate(rank, q) == q], key=near)
+    relay = sorted([a for a in far if gate(a, rank) == rank], key=near)
+    offe = topo.engines(core, cores[far[0]])
+    one = [e for e in topo.engines(core, cores[mate[0]]) if e not in offe]
+    h4, q2 = len(offe) // 2, len(offe) // 4
+
+    def gslot(d):
+        return r("WIN", GB + (d - 1) * 384, GB + d * 384)
+
+    dma("y", r("CI"), hb(T.cur0[:, :]), "ld0")
+    dma("y", r("CD", 0, 512), hb(T.cand[:, 0:512]), "ld1")
+    dma("s", r("CD", 512, 1024), hb(T.cand[:, 512:1024]), "ld2")
+    dma("s", r("CV"), hb(T.cov[:, :]), "ld3")
+    dma("y", r("SI"), hb(T.shown[:, :]), "ld4")
+    add("g", lambda: g.iota(T.PI[:, 0:1], [[0, 1]], 0, 1), [r("PI", 0, 1)], [])
+    iota(kf(0), [[2, 8], [-1, 2], [16, 8]], 1, 0)
+    iota(w(cIO), [[16, 128]], 0, 1)
+    iota(kf(2), [[1, 128]], 0, 0)
+    iota(kf(1), [[2, 64], [-1, 2]], 1, 0)
+    iota(r("NA", 0, 2048), [[-8, 16], [1, 8], [8, 16]], 0, 0)
+    iota(kf(3), [[1, 8], [0, 16]], 0, 0)
+    ms(r("XH"), 0.0)
+    act(r("H", 0, 2048), r("XH"), AF.Copy)
+    act(r("H", 2048, HG + 896), r("XH", 0, HG + 896 - 2048), AF.Copy)
+    ms(r("XL"), 0.0)
+    for i in range(8):
+        dma("y", r("XS", i * NP, (i + 1) * NP, p=slice(i, 128, 16)), r("H", 0, NP, p=slice(i, 128, 16)), "xz")
+    pc = [r("PC", k, k + 1) for k in range(8)]
+
+    def mask(t):
+        ts(r("PM", t * 128, (t + 1) * 128), r("CI"), float((t - 2) % 8), ALU.is_equal)
+
+    def names(k, dst):
+        c0 = (2 - k) * 128
+        tt(r("A1", 0, 512), r("CD", 0, 512), r("PM", c0, c0 + 512), ALU.mult)
+        tt(r("PX"), r("CD", 512, 1024), r("PM", c0 + 512, c0 + 1024), ALU.mult)
+        tt(r("A1", 1024, 1536), r("A1", 0, 512), r("PX"), ALU.add)
+        tt(r("A1", 1536, 1792), r("A1", 1024, 1280), r("A1", 1280, 1536), ALU.add)
+        tt(w(dst), r("A1", 1536, 1664), r("A1", 1664, 1792), ALU.add)
+
+    def split(src, half):
+        tc(wi(0), w(src))
+        ts(wi(1), wi(0), 15, ALU.bitwise_and)
+        ts(wi(2), wi(0), 1, ALU.bitwise_and)
+        tt(bl(0), w(src), wi(1), ALU.subtract)
+        if half:
+            tt(bl(1), w(cUH), wi(1), ALU.add)
+        tc(bl(2), wi(1))
+
+    def lists(src):
+        ts(bl(3), wi(2), -256.0, ALU.mult, 128.0, ALU.add)
+        ts(bl(4), w(src), 2048.0, ALU.is_ge, 4096.0, ALU.mult)
+        mms(r("PX", 256, 384), [(kb(6), bl(0)), (kb(7), bl(2)), (kb(5), bl(3)), (kb(5), bl(4))])
+        tt(w(t6), w(src), w(cIO), ALU.is_equal)
+        act(w(t7), w(t6), AF.Copy, scale=8192.0)
+        act(w(cDD), bl(0), AF.Copy, bias=-2032.0)
+        act(w(cDD + 1), bl(2), AF.Copy, bias=-16.0)
+        ts(of(oBX), r("PX", 256, 384), 2175.0, ALU.min)
+        if src == cB:
+            tc(w(cBX), r("PX", 256, 384))
+        else:
+            tt(w(cDX), w(cBX), r("PX", 256, 384), ALU.subtract)
+        tt(w(cEC), w(t7), w(cIO), ALU.add)
+
+    for t in range(2, 10):
+        mask(t)
+    tc(pc[0], r("PI", 0, 1))
+    ts(r("PI", 1, 2), r("PI", 0, 1), 4, ALU.arith_shift_right)
+    ts(r("XH", 0, 2048, 16), kf(0), pc[0], ALU.is_equal)
+    ts(r("XL", 1, 2048, 16), kf(0), pc[0], ALU.is_equal)
+    tc(pc[1], r("PI", 1, 2))
+    names(0, cB)
+    split(cB, False)
+    act(r("X0", 0, 2048, 2), r("CV"), AF.Copy, bias=4064.0)
+    act(r("X0", 1, 2048, 2), r("CV"), AF.Copy, bias=4064.0)
+    expand(bl(0), bl(2), "WP", ALT)
+    act(r("X1", 0, 2048, 2), r("CV"), AF.Copy, bias=4064.0)
+    act(r("X1", 1, 2048, 2), r("CV"), AF.Copy, bias=4064.0)
+    ts(pc[2], pc[1], -16.0, ALU.mult)
+    for k, s in ((5, 1.0), (6, 0.0625), (7, 128.0)):
+        ts(kb(k), kf(2), pc[0], ALU.is_equal, s, ALU.mult)
+    ts(w(cIO), w(cIO), pc[2], ALU.add)
+    ms(r("WP", 2048, 2176), 128.0)
+    lists(cB)
+    ts(r("EX"), r("NA", 0, 2048), pc[1], ALU.is_equal)
+    for h, q in ((0, "v"), (1, "s"), (2, "v"), (3, "s")):
+        tc(r("NB", h * 512, (h + 1) * 512), ind(r("WP"), of(oBX, h * 32, (h + 1) * 32)), q)
+        if h % 2:
+            ext("NB", (h // 2) * 1024, 64, r("PB" if h == 1 else "PY", 0, 64))
+    for k, s in enumerate((1.0, 0.0625, 128.0)):
+        ts(kb(k), kf(1), pc[0], ALU.is_equal, s, ALU.mult)
+    ms(r("X0", 2048, 2064), 0.0)
+    ms(r("WN", 2048, 2176), 128.0)
+    for h in range(2):
+        tt(wh(cP0, h), r("PB" if h == 0 else "PY", 0, 64), wh(cEC, h), ALU.is_equal)
+    tt(r("PA", 0, 128), w(cP0), w(cDD), ALU.mult)
+    tt(r("PA", 128, 256), w(cP0), w(cDD + 1), ALU.mult)
+    ts(hl(0), r("PA", 0, 128), 2032.0, ALU.add)
+    ts(hl(1), r("PA", 128, 256), 16.0, ALU.add)
+    sm = [r("SM", k * 8, k * 8 + 8) for k in range(8)]
+
+    def constants_a():
+        si = r("SI")
+        pi = [r("WI", 384 + k * 8, 392 + k * 8) for k in range(4)]
+        for nm in ("UA", "UB"):
+            ms(r(nm, 2048, 2064), 0.0)
+        for nm in ("NA", "NB"):
+            ms(r(nm, 2048, 2064), 128.0)
+        ts(pi[1], si, 14, ALU.bitwise_and)
+        ts(pi[2], si, 1, ALU.bitwise_and)
+        ts(pi[0], si, 4, ALU.arith_shift_right)
+        ts(sm[0], pi[1], 128.0, ALU.mult, 128.0, ALU.add)
+        ts(sm[1], pi[2], -128.0, ALU.mult)
+        tc(r("OP", 0, 8), si)
+        tt(sm[0], sm[0], pi[0], ALU.add)
+        ts(sm[4], si, -2048.0, ALU.add)
+        ts(pc[3], pc[0], 96.0, ALU.add)
+        tt(sm[0], sm[0], sm[1], ALU.add)
+        ts(pc[4], pc[3], 128.0, ALU.is_ge, -128.0, ALU.mult)
+        tc(r("OP", 32, 40), sm[0])
+        tt(pc[3], pc[3], pc[4], ALU.add)
+        mask(0)
+        mask(1)
+        ts(kf(4), kf(2), pc[3], ALU.is_equal)
+
+    def constants_b():
+        ts(pc[5], pc[1], 6.0, ALU.is_ge, -8.0, ALU.mult)
+        ts(pc[6], pc[1], 2.0, ALU.add)
+        ts(kb(3), kf(3), pc[1], ALU.is_equal)
+        tt(pc[6], pc[6], pc[5], ALU.add)
+        ms(r("TT", 2048, 2064), 0.0)
+        act(r("H2"), r("H", 0, E), AF.Copy)
+        ts(kb(4), kf(3), pc[6], ALU.is_equal)
+
+    def slots():
+        ts(w(t3), r("CI"), float(NP), ALU.mult)
+        tc(of(oBM), w(cB))
+        tt(w(t3), w(t3), w(cB), ALU.add)
+        act(w(t4), w(cB), AF.Copy, scale=3.0, bias=-4096.0)
+        ts(w(t5), w(cB), 2047.5, ALU.is_lt, float(AO - 1), ALU.mult)
+        tc(of(oX), w(t3))
+
+    for rnd in range(3):
+        last = rnd == 2
+        wt = 2.0 ** (24 * rnd)
+        mms(r("PX", 0, 128), [(kb(0), hl(0)), (kb(0), hl(1))])
+        mms(r("PX", 128, 256), [(kb(1), hl(0)), (kb(2), hl(1))])
+        tc(r("OF", 0, 256), r("PX", 0, 256))
+        expand(hl(0), hl(1), "WN", ALT if rnd == 0 else PMB)
+        ub = ["X0", "UA", "UB", "UA", "UB", "UA", "WIN"]
+        nb = ["WN", "NA", "NB", "NA", "NB", "NA"]
+
+        def twin(t, c):
+            o, a = r("MH", c * 512, (c + 1) * 512), r(ub[t], c * 512, (c + 1) * 512)
+            if c == 3:
+                tc(o, a, "s")
+            else:
+                add("g", lambda: g.affine_select(o["ap"], a["ap"], [[0, 512]], ALU.is_ge, 0.0, 0, 0), [o], [a])
+
+        def ustep(t, lo, hi):
+            for c in range(lo // 512, hi // 512):
+                tt(r(ub[t], c * 512, (c + 1) * 512), ind(r(ub[t - 1], 0, 2064), of(oN[t - 1], c * 32, c * 32 + 32)),
+                   r("X1" if t == 1 else "MH", c * 512, (c + 1) * 512), ALU.add)
+                if t < 6 and c < 3:
+                    twin(t, c)
+
+        def nstep(k, h):
+            tc(r(nb[k], h * 1024, (h + 1) * 1024), ind(r(nb[k - 1]), of(o1 if k == 1 else oN[k - 1], h * 64, h * 64 + 64)), "s")
+            if h == 0 and k > 1:
+                twin(k - 1, 3)
+            if (k, h) != (5, 1):
+                ext(nb[k], h * 1024, 64, r("PX" if h == 0 else "PY", 0, 64))
+
+        def conv(k, h):
+            tc(of(oN[k], h * 64, h * 64 + 64), r("PX" if h == 0 else "PY", 0, 64))
+
+        def small(j, win, lo, n):
+            tc(r("SG", j * 256, j * 256 + 16 * n), ind(r(win), r("OP", lo, lo + n)), "s")
+            ext("SG", j * 256, n, r("PA", j * 16, j * 16 + n))
+
+        ustep(1, 0, 2048)
+        if rnd == 0:
+            constants_a()
+            names(1, cR1)
+        else:
+            mv = r("PB", 0, 128)
+            tt(w(t0), w(cDB), mv, ALU.mult)
+            tt(w(t2), w(cDX), mv, ALU.mult)
+            tt(wi(4), r("CI"), mv, ALU.add)
+            if rnd == 1:
+                tt(w(t1), w(cR2), mv, ALU.mult)
+            tt(w(cB), w(cB), w(t0), ALU.add)
+            tt(w(cBX), w(cBX), w(t2), ALU.subtract)
+            ts(r("CI"), wi(4), 7, ALU.bitwise_and)
+            ts(of(oBX), w(cBX), 2175.0, ALU.min)
+            if rnd == 1:
+                tt(w(cBP), w(t1), w(cR1), ALU.add)
+        nstep(1, 0)
+        nstep(1, 1)
+        for k in range(1, 5):
+            conv(k, 0)
+            if k == 4:
+                small(1, "NB", 0, 16)
+            nstep(k + 1, 0)
+            ustep(k + 1, 0, 1024)
+            conv(k, 1)
+            if k == 1:
+                small(0, "WN", 32, 8)
+            if k == 4:
+                tc(r("OP", 48, 64), r("PA", 16, 32))
+                small(2, "NB", 48, 16)
+            nstep(k + 1, 1)
+            ustep(k + 1, 1024, 2048)
+            if k == 1:
+                ts(sm[3], r("PA", 0, 8), 2047.5, ALU.is_ge)
+                tc(r("OP", 8, 16), r("PA", 0, 8))
+                tt(sm[3], sm[3], sm[4], ALU.mult)
+            if k == 2:
+                tt(sm[3], sm[3], r("PA", 0, 8), ALU.add)
+            if k == 3:
+                tc(r("OP", 40, 48), sm[3])
+        tc(r("OP", 16, 32), r("PA", 32, 48))
+        tc(r("PG", 0, 256), ind(r("UA"), r("OP", 0, 16)))
+        conv(5, 0)
+        tt(r("PG", 256, 512), ind(r("UA"), r("OP", 16, 32)), r("PG", 0, 256), ALU.add)
+        mm(r("PB", 0, 256), kf(4), r("PG", 256, 512), True, True)
+        ext("NA", 1024, 64, r("PY", 0, 64))
+        twin(5, 3)
+        tc(r("NB", 0, 2048), ind(r("WN"), of(oBX)), "s")
+        ustep(6, 0, 512)
+        ts(r("PF", 0, 256), r("PB", 0, 256), MAGIC, ALU.add, -MAGIC, ALU.add)
+        tc(r("PAY", 0, 384, 3), r("PB", 0, 128))
+        tt(r("PF", 256, 384), r("PF", 128, 256), r("PB", 0, 128), ALU.mult)
+        tt(r("PA", 128, 256), r("PF", 0, 128), r("PB", 128, 256), ALU.mult)
+        tc(r("PAY", 2, 384, 3), r("PF", 128, 256))
+        tt(r("PAY", 1, 384, 3), r("PF", 256, 384), r("PA", 128, 256), ALU.subtract)
+
+        def out(q, es):
+            d = (q - rank) % NR
+            return (cores[q], r("PAY"), gslot(d), "ga%d" % d, es)
+        send([out(q, offe[j * h4:(j + 1) * h4]) for j, q in enumerate(direct[:2])] + [out(q, one) for q in mate], "sent")
+        send([out(q, offe) for q in direct[2:]], "sent")
+        order = mate + relay + [a for a in far if a not in relay]
+        for a in order:
+            d = (rank - a) % NR
+            arrive("ga%d" % d, len(one) if a not in relay else (len(offe) if near(a) else h4), gslot(d))
+        fw = []
+        for a in relay:
+            d2 = (mate[0] - a) % NR
+            fw.append(send([(cores[mate[0]], gslot((rank - a) % NR), gslot(d2), "ga%d" % d2, one)], "fwd"))
+        conv(5, 1)
+        ustep(6, 512, 2048)
+        ext("NB", 0, 128, r("PX", 0, 128))
+        mms(r("PX", 128, 256), [(kb(5), hl(0)), (kb(5), hl(1))])
+        if rnd == 0:
+            names_px = r("PY")
+            tt(r("A1", 0, 512), r("CD", 0, 512), r("PM", 0, 512), ALU.mult)
+            tt(names_px, r("CD", 512, 1024), r("PM", 512, 1024), ALU.mult)
+            tt(r("A1", 1024, 1536), r("A1", 0, 512), names_px, ALU.add)
+        for h in range(2):
+            ts(r("WIN", MO + h * 1024, MO + (h + 1) * 1024), r("WIN", h * 1024, (h + 1) * 1024), MAGIC, ALU.add, -MAGIC, ALU.add)
+            tc(r("PM", h * 1024, (h + 1) * 1024), r("WIN", MO + h * 1024, MO + (h + 1) * 1024), "s")
+        slots()
+        if rnd == 0:
+            constants_b()
+            tt(r("A1", 1536, 1792), r("A1", 1024, 1280), r("A1", 1280, 1536), ALU.add)
+            tc(w(cBP), w(cR1))
+            tt(w(cR2), r("A1", 1536, 1664), r("A1", 1664, 1792), ALU.add)
+        tt(w(t4), w(t4), w(cB), ALU.max)
+        tc(of(oPT), r("PX", 128, 256))
+        tt(w(t5), w(t5), w(t4), ALU.add)
+        tc(of(oBU), w(t4))
+        ts(w(t0), w(t5), float(2 - MO), ALU.add)
+        ts(of(oR), w(t5), float(1 - GB), ALU.add)
+        tt(w(t0), w(t0), r("PX", 0, 128), ALU.min)
+        ts(bl(5), hl(1), 16.0, ALU.is_equal, wt, ALU.mult)
+        ts(of(oH), w(t0), float(MO - GB), ALU.add)
+        ms(r("PC", 7, 8), -8.0 * wt)
+        if last:
+            for c in range(4):
+                pn = "PA" if c % 2 == 0 else "PB"
+                act(r(pn), r("WIN", MO + c * 512, MO + (c + 1) * 512), AF.Copy, scale=-4064.0 / 4096.0)
+                tt(r("UB", c * 512, (c + 1) * 512, 2), r("WIN", c * 512 + 1, (c + 1) * 512, 2), r(pn, 1, 512, 2), ALU.add)
+                tt(r("UB", c * 512 + 1, (c + 1) * 512, 2), r("WIN", c * 512, (c + 1) * 512, 2), r(pn, 0, 512, 2), ALU.add)
+        else:
+            ts(w(cUH), hl(1), 16.0, ALU.is_equal, 0.5, ALU.mult)
+            if rnd == 0:
+                tt(w(cR2), w(cR2), w(cR1), ALU.subtract)
+            split(cBP, True)
+        for a in order:
+            d = (rank - a) % NR
+            kd = ts(r("WIN", MF + (d - 1) * 128, MF + d * 128), r("WIN", GB + (d - 1) * 384, GB + d * 384, 3), MAGIC, ALU.add, -MAGIC, ALU.add)
+        if last:
+            dma("y", hb(T.ys[:, :]), r("UB", 0, 2048), "oy", after=[kd])
+
+        def ch(nm, c, base=0):
+            return r(nm, base + c * 512, base + (c + 1) * 512)
+
+        def oc(k, c):
+            return of(k, c * 32, c * 32 + 32)
+
+        def alt(c):
+            return r("PB" if c % 2 == 0 else "PY")
+
+        def own(c):
+            return r("PA" if c % 2 == 0 else "PX")
+
+        def gub(c):
+            act(ch("UA", c), ind(r("WIN", 0, MO), oc(oBU, c)), AF.Identity)
+
+        def gmh(c):
+            act(ch("MH", c), ind(r("WIN", GB, AO), oc(oH, c)), AF.Identity)
+
+        def a1(c):
+            tt(ch("A1", c), ind(r("WIN", MO, AO), oc(oBM, c)), ch("WIN", c), ALU.mult)
+
+        def bym(c):
+            tt(own(c), ch("UA", c), ch("PM", c), ALU.mult)
+
+        def dif(c):
+            tt(ch("WIN", c, AO), ch("A1", c), own(c), ALU.subtract)
+
+        def sabs(c):
+            act(alt(c), ch("WIN", c, AO), AF.Abs)
+
+        def left(c):
+            tt(ch("A1", c), ch("MH", c), alt(c), ALU.mult)
+
+        def gg(c):
+            act(ch("UA", c), ind(r("WIN", GB, WE), oc(oR, c)), AF.Abs)
+
+        def vote(c):
+            tt(ch("NA", c), ch("A1", c), own(c), ALU.is_lt)
+            mm(alt(c), kb(3), ch("NA", c), True, True)
+
+        def evac(c):
+            act(ch("NB", c), alt(c), AF.Relu, scale=wt, bias=r("PC", 7, 8))
+
+        def scat(c):
+            tc(ind(r("XS"), oc(oX, c)), ch("NB", c))
+
+        gub(0); gub(1); a1(0); bym(0); a1(1); dif(0); gmh(0); gub(2); bym(1); a1(2); dif(1); sabs(0); gub(3); left(0)
+        gmh(1); sabs(1); bym(2); a1(3); dif(2); left(1); gmh(2); bym(3); gmh(3); sabs(2); dif(3); left(2)
+        gg(0); sabs(3); bym(0); left(3); gg(1); bym(1); vote(0); gg(2); evac(0); vote(1); bym(2); gg(3); evac(1); scat(0)
+        vote(2); bym(3); evac(2); scat(1); vote(3); evac(3); scat(2); scat(3)
+
+        for i in range(8):
+            dma("y", r("H", HG, HG + 896, p=slice(i, 128, 16)), r("XS", i * NP + E, (i + 1) * NP, p=slice(i, 128, 16)), "dg")
+        for i in range(8):
+            for nm in ("H", "H2"):
+                dma("y", r(nm, 0, E, p=slice(i, 128, 16)), r("XS", i * NP, i * NP + E, p=slice(i, 128, 16)), "do")
+
+        def back(q, es):
+            d = (rank - q) % NR
+            return (cores[q], r("H", HG + (d - 1) * 128, HG + d * 128), r("RET", (d - 1) * 128, d * 128), "ret", es)
+        fo = sorted(far, key=lambda q: (q - rank) % NR)
+        send([back(q, offe[j * q2:(j + 1) * q2]) for j, q in enumerate(fo[:4])] + [back(q, one) for q in mate], "rsent", after=fw)
+        send([back(q, offe[j * h4:(j + 1) * h4]) for j, q in enumerate(fo[4:])], "rsent")
+        tot = len(one)
+        for a in far:
+            fa = sorted([x for x in range(NR) if topo.chip(cores[x]) != topo.chip(cores[a])], key=lambda x: (x - a) % NR)
+            tot += q2 if fa.index(rank) < 4 else h4
+        arrive("ret", tot, r("RET"))
+        if not last:
+            expand(bl(0), bl(1), "WP", PMB)
+            lists(cBP)
+            ts(of(oT2), w(cBP), 2048.0, ALU.min)
+            tt(w(cDB), w(cBP), w(cB), ALU.subtract)
+            for h in range(2):
+                tc(r("NB", h * 1024, (h + 1) * 1024), ind(r("WP"), of(oBX, h * 64, h * 64 + 64)), "s")
+                ext("NB", h * 1024, 64, r("PB" if h == 0 else "PY", 0, 64))
+            act(w(cB0), hl(0), AF.Copy, bias=-2032.0)
+            act(w(cB0 + 1), hl(1), AF.Copy, bias=-16.0)
+        tt(r("TT", 0, E), ind(r("H", 0, HG), of(oPT)), r("H2"), ALU.add)
+        tc(r("RV", 0, 128), ind(r("TT"), r("OP", 0, 8)))
+        if not last:
+            for h in range(2):
+                tt(wh(cD, h), r("PB" if h == 0 else "PY", 0, 64), wh(cEC, h), ALU.subtract)
+            ts(r("PB", 128, 256), w(cD), 0.5, ALU.is_equal)
+            ts(r("PB", 256, 384), w(cD), 0.0, ALU.is_equal)
+            for h in range(2):
+                tt(w(cE1 + h), w(cDD + h), r("PB", 128, 256), ALU.mult)
+            for h in range(2):
+                tt(w(cE2 + h), w(cDD + h), r("PB", 256, 384), ALU.mult)
+            tt(w(cE1, 2), w(cE1, 2), w(cB0, 2), ALU.subtract)
+        mms(r("PA", 0, 128), [(kb(4), r("RET", (d - 1) * 128, d * 128)) for d in range(1, NR)])
+        tt(r("RV", 128, 256), r("RV", 0, 128), r("PA", 0, 128), ALU.add)
+        tc(r("RV", 256, 384), r("PA", 0, 128), "s")
+        tc(ind(r("TT"), r("OP", 0, 8)), r("RV", 128, 256))
+        tt(r("RV", 384, 512), ind(r("TT"), r("OP", 40, 48)), r("RV", 256, 384), ALU.add)
+        tc(ind(r("TT"), r("OP", 40, 48)), r("RV", 384, 512))
+        ext("TT", 0, 128, r("PX", 0, 128), more=[(kb(5), bl(5))])
+        mv = r("PB", 0, 128)
+        if not last:
+            for h, q in ((0, "v"), (1, "s"), (2, "v"), (3, "s")):
+                tc(ch("NA", h), ind(r("TT"), oc(oT2, h)), q)
+            for h in range(2):
+                ext("NA", h * 1024, 64, r("PY", h * 64, h * 64 + 64))
+        ts(mv, r("PX", 0, 128), 0.5 * wt, ALU.is_ge)
+        if not last:
+            for h in range(2):
+                tt(r("PB", 128 + h * 128, 256 + h * 128), w(cE1 + h), mv, ALU.mult)
+            for h in range(2):
+                tt(w(cDL + h), w(cE2 + h), mv, ALU.mult)
+            tt(w(cB0, 2), r("HL"), r("PB", 128, 384), ALU.add)
+            ts(r("PA", 0, 128), r("PY", 0, 128), 0.5 * wt, ALU.is_ge)
+            for h in range(2):
+                tt(r("PA", 128 + h * 128, 256 + h * 128), w(cDL + h), r("PA", 0, 128), ALU.mult)
+            tt(r("HL"), w(cB0, 2), r("PA", 128, 384), ALU.add)
+        else:
+            tt(wi(4), r("CI"), mv, ALU.add)
+            ts(wi(0), wi(4), 7, ALU.bitwise_and)
+            tc(w(t0), wi(0))
+            dma("y", hb(T.yc[:, :]), w(t0), "oc")
+
+    csem = {"v": "cv", "s": "cs", "t": "ct", "g": "cg"}
+    pos, clock, need = {}, {}, set()
+    seen = {q: {} for q in Q}
+    plan = []
+    for k, o in enumerate(ops):
+        q = o["q"]
+        if q == "x":
+            clock[k] = {o["sem"]: o["tot"]}
+            plan.append(None)
+            continue
+        kn = seen[q]
+        ws = []
+        for j in sorted(o["deps"], reverse=True):
+            p = ops[j]
+            if p["kind"] == "c":
+                key, val = "#" + p["q"], j
+            else:
+                key, val = p["sem"], o["waits"][p["sem"]]
+            if kn.get(key, -1) >= val:
+                continue
+            ws.append((key, val))
+            kn[key] = val
+            if p["kind"] == "c":
+                need.add(j)
+            for a, b in clock[j].items():
+                if kn.get(a, -1) < b:
+                    kn[a] = b
+        clock[k] = dict(kn)
+        plan.append(ws)
+    num = {q: 0 for q in csem}
+    for k, o in enumerate(ops):
+        if k in need:
+            num[o["q"]] += 1
+            pos[k] = num[o["q"]]
+    for k, o in enumerate(ops):
+        if o["q"] == "x":
+            continue
+        for key, val in plan[k]:
+            if key[0] == "#":
+                Q[o["q"]].wait_ge(T.sem[csem[key[1]]], pos[val])
+            else:
+                Q[o["q"]].wait_ge(T.sem[key], val)
+        ins = o["fn"]()
+        if k in need:
+            ins.then_inc(T.sem[csem[o["q"]]], 1)
+    for s in sorted(cnt):
+        if max(seen[q].get(s, 0) for q in Q) < cnt[s]:
+            g.wait_ge(T.sem[s], cnt[s])

@@ -8,7 +8,7 @@ F, B, I, U = "float32", "bfloat16", "int32", "uint16"
 SCRATCH = {
     "WIN": ("sbuf", [128, WE], F), "X0": ("sbuf", [128, 2064], F), "UA": ("sbuf", [128, 2064], F),
     "UB": ("sbuf", [128, 2064], F), "MH": ("sbuf", [128, 2048], F), "A1": ("sbuf", [128, 2048], F),
-    "X1": ("sbuf", [128, 2048], F), "H2": ("sbuf", [128, 2048], B), "XS": ("sbuf", [128, 8 * NP], B), "H": ("sbuf", [128, HG + 896], B), "TT": ("sbuf", [128, 2064], B),
+    "X1": ("sbuf", [128, 2048], F), "H2": ("sbuf", [128, HG], B), "XS": ("sbuf", [128, 8 * NP], B), "H": ("sbuf", [128, HG + 896], B), "TT": ("sbuf", [128, 2064], B),
     "WN": ("sbuf", [128, 2176], B), "WP": ("sbuf", [128, 2176], B), "NA": ("sbuf", [128, 2064], B), "NB": ("sbuf", [128, 2064], B),
     "EX": ("sbuf", [128, 2048], B), "XH": ("sbuf", [128, 2048], B), "XL": ("sbuf", [128, 2048], B),
     "CV": ("sbuf", [128, 1024], B), "CD": ("sbuf", [128, 1024], I), "CI": ("sbuf", [128, 128], I), "SI": ("sbuf", [128, 8], I),
@@ -20,7 +20,7 @@ SCRATCH = {
     "PM": ("psum", [128, 2048], F), "PA": ("psum", [128, 512], F), "PB": ("psum", [128, 512], F),
     "PX": ("psum", [128, 512], F), "PY": ("psum", [128, 512], F),
 }
-SEMAPHORES = ["cv", "cs", "ct", "cg", "ld0", "ld1", "ld2", "ld3", "ld4", "xz", "dg", "do", "oy", "oc", "sent", "fwd", "rsent", "ret"] + \
+SEMAPHORES = ["cv", "cs", "ct", "cg", "ld0", "ld1", "ld2", "ld3", "ld4", "xz", "tw0", "tw1", "tw2", "tw3", "dg", "do", "oy", "oc", "sent", "fwd", "rsent", "ret"] + \
              ["ga%d" % d for d in range(1, 8)]
 
 
@@ -177,8 +177,12 @@ def rank_program(g, core, T, topo):
 
     def near(q):
         return topo.mates(topo.chip(core), topo.chip(cores[q]))
-    direct = sorted([q for q in far if gate(rank, q) == q], key=near)
-    relay = sorted([a for a in far if gate(a, rank) == rank], key=near)
+
+    def planar(q):
+        return topo.same_plane(topo.chip(core), topo.chip(cores[q]))
+    both = [q for q in far if near(q)]
+    direct = sorted([q for q in far if gate(rank, q) == q and not near(q)], key=planar)
+    relay = sorted([a for a in far if gate(a, rank) == rank and not near(a)], key=planar)
     offe = topo.engines(core, cores[far[0]])
     one = [e for e in topo.engines(core, cores[mate[0]]) if e not in offe]
     h4, q2 = len(offe) // 2, len(offe) // 4
@@ -204,6 +208,7 @@ def rank_program(g, core, T, topo):
     ms(r("XL"), 0.0)
     for i in range(8):
         dma("y", r("XS", i * NP, (i + 1) * NP, p=slice(i, 128, 16)), r("H", 0, NP, p=slice(i, 128, 16)), "xz")
+    dma("y", r("H2"), r("H", 0, HG), "xz")
     pc = [r("PC", k, k + 1) for k in range(8)]
 
     def mask(t):
@@ -252,16 +257,15 @@ def rank_program(g, core, T, topo):
     split(cB, False)
     act(r("X0", 0, 2048, 2), r("CV"), AF.Copy, bias=4064.0)
     act(r("X0", 1, 2048, 2), r("CV"), AF.Copy, bias=4064.0)
+    dma("y", r("X1"), r("X0", 0, 2048), "tw0")
     expand(bl(0), bl(2), "WP", ALT)
-    act(r("X1", 0, 2048, 2), r("CV"), AF.Copy, bias=4064.0)
-    act(r("X1", 1, 2048, 2), r("CV"), AF.Copy, bias=4064.0)
     ts(pc[2], pc[1], -16.0, ALU.mult)
     for k, s in ((5, 1.0), (6, 0.0625), (7, 128.0)):
         ts(kb(k), kf(2), pc[0], ALU.is_equal, s, ALU.mult)
     ts(w(cIO), w(cIO), pc[2], ALU.add)
     ms(r("WP", 2048, 2176), 128.0)
-    lists(cB)
     ts(r("EX"), r("NA", 0, 2048), pc[1], ALU.is_equal)
+    lists(cB)
     for h, q in ((0, "v"), (1, "s"), (2, "v"), (3, "s")):
         tc(r("NB", h * 512, (h + 1) * 512), ind(r("WP"), of(oBX, h * 32, (h + 1) * 32)), q)
         if h % 2:
@@ -270,6 +274,8 @@ def rank_program(g, core, T, topo):
         ts(kb(k), kf(1), pc[0], ALU.is_equal, s, ALU.mult)
     ms(r("X0", 2048, 2064), 0.0)
     ms(r("WN", 2048, 2176), 128.0)
+    mask(0)
+    mask(1)
     for h in range(2):
         tt(wh(cP0, h), r("PB" if h == 0 else "PY", 0, 64), wh(cEC, h), ALU.is_equal)
     tt(r("PA", 0, 128), w(cP0), w(cDD), ALU.mult)
@@ -298,17 +304,15 @@ def rank_program(g, core, T, topo):
         ts(pc[4], pc[3], 128.0, ALU.is_ge, -128.0, ALU.mult)
         tc(r("OP", 32, 40), sm[0])
         tt(pc[3], pc[3], pc[4], ALU.add)
-        mask(0)
-        mask(1)
+        ts(kf(0), kf(2), pc[0], ALU.is_equal)
         ts(kf(4), kf(2), pc[3], ALU.is_equal)
 
     def constants_b():
         ts(pc[5], pc[1], 6.0, ALU.is_ge, -8.0, ALU.mult)
         ts(pc[6], pc[1], 2.0, ALU.add)
-        ts(kb(3), kf(3), pc[1], ALU.is_equal)
-        tt(pc[6], pc[6], pc[5], ALU.add)
         ms(r("TT", 2048, 2064), 0.0)
-        act(r("H2"), r("H", 0, E), AF.Copy)
+        tt(pc[6], pc[6], pc[5], ALU.add)
+        tt(w(cR2), w(cR2), w(cR1), ALU.subtract)
         ts(kb(4), kf(3), pc[6], ALU.is_equal)
 
     def slots():
@@ -331,24 +335,31 @@ def rank_program(g, core, T, topo):
 
         def twin(t, c):
             o, a = r("MH", c * 512, (c + 1) * 512), r(ub[t], c * 512, (c + 1) * 512)
-            if c == 3:
-                tc(o, a, "s")
+            if c % 2 == t % 2:
+                dma("y", o, a, "tw%d" % c)
             else:
                 add("g", lambda: g.affine_select(o["ap"], a["ap"], [[0, 512]], ALU.is_ge, 0.0, 0, 0), [o], [a])
 
         def ustep(t, lo, hi):
-            for c in range(lo // 512, hi // 512):
+            cs = list(range(lo // 512, hi // 512))
+            if t % 2:
+                cs = [c ^ 1 for c in cs]
+            for c in cs:
                 tt(r(ub[t], c * 512, (c + 1) * 512), ind(r(ub[t - 1], 0, 2064), of(oN[t - 1], c * 32, c * 32 + 32)),
                    r("X1" if t == 1 else "MH", c * 512, (c + 1) * 512), ALU.add)
-                if t < 6 and c < 3:
+                if t < 6:
                     twin(t, c)
 
         def nstep(k, h):
             tc(r(nb[k], h * 1024, (h + 1) * 1024), ind(r(nb[k - 1]), of(o1 if k == 1 else oN[k - 1], h * 64, h * 64 + 64)), "s")
-            if h == 0 and k > 1:
-                twin(k - 1, 3)
             if (k, h) != (5, 1):
                 ext(nb[k], h * 1024, 64, r("PX" if h == 0 else "PY", 0, 64))
+            if rnd == 0 and k in (2, 3):
+                for i in range(4 * h, 4 * h + 4):
+                    c0 = (k - 2) * 1024 + i * 128
+                    mm(r("PB", (k - 2) * 128, (k - 1) * 128), kf(0), r("A1", c0, c0 + 128), i == 0, i == 7)
+            if rnd == 0 and (k, h) == (5, 0):
+                tc(w(cR1, 2), r("PB", 0, 256), "s")
 
         def conv(k, h):
             tc(of(oN[k], h * 64, h * 64 + 64), r("PX" if h == 0 else "PY", 0, 64))
@@ -360,7 +371,8 @@ def rank_program(g, core, T, topo):
         ustep(1, 0, 2048)
         if rnd == 0:
             constants_a()
-            names(1, cR1)
+            for k in (1, 2):
+                tt(r("A1", (k - 1) * 1024, k * 1024), r("CD"), r("PM", (2 - k) * 128, (2 - k) * 128 + 1024), ALU.mult)
         else:
             mv = r("PB", 0, 128)
             tt(w(t0), w(cDB), mv, ALU.mult)
@@ -404,7 +416,6 @@ def rank_program(g, core, T, topo):
         tt(r("PG", 256, 512), ind(r("UA"), r("OP", 16, 32)), r("PG", 0, 256), ALU.add)
         mm(r("PB", 0, 256), kf(4), r("PG", 256, 512), True, True)
         ext("NA", 1024, 64, r("PY", 0, 64))
-        twin(5, 3)
         tc(r("NB", 0, 2048), ind(r("WN"), of(oBX)), "s")
         ustep(6, 0, 512)
         ts(r("PF", 0, 256), r("PB", 0, 256), MAGIC, ALU.add, -MAGIC, ALU.add)
@@ -417,12 +428,13 @@ def rank_program(g, core, T, topo):
         def out(q, es):
             d = (q - rank) % NR
             return (cores[q], r("PAY"), gslot(d), "ga%d" % d, es)
-        send([out(q, offe[j * h4:(j + 1) * h4]) for j, q in enumerate(direct[:2])] + [out(q, one) for q in mate], "sent")
-        send([out(q, offe) for q in direct[2:]], "sent")
-        order = mate + relay + [a for a in far if a not in relay]
+        for j, q in enumerate(direct):
+            send([out(q, offe)] + [out(x, one) for x in mate if j == 0], "sent")
+        send([out(q, offe[j * h4:(j + 1) * h4]) for j, q in enumerate(both)], "sent")
+        order = mate + relay + both + [a for a in far if a not in relay + both]
         for a in order:
             d = (rank - a) % NR
-            arrive("ga%d" % d, len(one) if a not in relay else (len(offe) if near(a) else h4), gslot(d))
+            arrive("ga%d" % d, h4 if a in both else (len(offe) if a in relay else len(one)), gslot(d))
         fw = []
         for a in relay:
             d2 = (mate[0] - a) % NR
@@ -431,20 +443,15 @@ def rank_program(g, core, T, topo):
         ustep(6, 512, 2048)
         ext("NB", 0, 128, r("PX", 0, 128))
         mms(r("PX", 128, 256), [(kb(5), hl(0)), (kb(5), hl(1))])
-        if rnd == 0:
-            names_px = r("PY")
-            tt(r("A1", 0, 512), r("CD", 0, 512), r("PM", 0, 512), ALU.mult)
-            tt(names_px, r("CD", 512, 1024), r("PM", 512, 1024), ALU.mult)
-            tt(r("A1", 1024, 1536), r("A1", 0, 512), names_px, ALU.add)
-        for h in range(2):
-            ts(r("WIN", MO + h * 1024, MO + (h + 1) * 1024), r("WIN", h * 1024, (h + 1) * 1024), MAGIC, ALU.add, -MAGIC, ALU.add)
-            tc(r("PM", h * 1024, (h + 1) * 1024), r("WIN", MO + h * 1024, MO + (h + 1) * 1024), "s")
+        ts(r("WIN", MO + 1536, MO + 2048), r("WIN", 1536, 2048), MAGIC, ALU.add, -MAGIC, ALU.add)
         slots()
+        for lo, hi in ((0, 1024), (1024, 1536)):
+            act(r("MH", lo, hi), r("WIN", lo, hi), AF.Copy, bias=MAGIC)
+            act(r("WIN", MO + lo, MO + hi), r("MH", lo, hi), AF.Copy, bias=-MAGIC)
+            act(r("PM", lo, hi), r("MH", lo, hi), AF.Copy, bias=-MAGIC)
+        tc(r("PM", 1536, 2048), r("WIN", MO + 1536, MO + 2048), "s")
         if rnd == 0:
-            constants_b()
-            tt(r("A1", 1536, 1792), r("A1", 1024, 1280), r("A1", 1280, 1536), ALU.add)
-            tc(w(cBP), w(cR1))
-            tt(w(cR2), r("A1", 1536, 1664), r("A1", 1664, 1792), ALU.add)
+            ts(kb(3), kf(3), pc[1], ALU.is_equal)
         tt(w(t4), w(t4), w(cB), ALU.max)
         tc(of(oPT), r("PX", 128, 256))
         tt(w(t5), w(t5), w(t4), ALU.add)
@@ -452,25 +459,15 @@ def rank_program(g, core, T, topo):
         ts(w(t0), w(t5), float(2 - MO), ALU.add)
         ts(of(oR), w(t5), float(1 - GB), ALU.add)
         tt(w(t0), w(t0), r("PX", 0, 128), ALU.min)
-        ts(bl(5), hl(1), 16.0, ALU.is_equal, wt, ALU.mult)
-        ts(of(oH), w(t0), float(MO - GB), ALU.add)
         ms(r("PC", 7, 8), -8.0 * wt)
-        if last:
-            for c in range(4):
-                pn = "PA" if c % 2 == 0 else "PB"
-                act(r(pn), r("WIN", MO + c * 512, MO + (c + 1) * 512), AF.Copy, scale=-4064.0 / 4096.0)
-                tt(r("UB", c * 512, (c + 1) * 512, 2), r("WIN", c * 512 + 1, (c + 1) * 512, 2), r(pn, 1, 512, 2), ALU.add)
-                tt(r("UB", c * 512 + 1, (c + 1) * 512, 2), r("WIN", c * 512, (c + 1) * 512, 2), r(pn, 0, 512, 2), ALU.add)
-        else:
+        ts(of(oH), w(t0), float(MO - GB), ALU.add)
+        if not last:
             ts(w(cUH), hl(1), 16.0, ALU.is_equal, 0.5, ALU.mult)
-            if rnd == 0:
-                tt(w(cR2), w(cR2), w(cR1), ALU.subtract)
-            split(cBP, True)
+            nxt = cR1 if rnd == 0 else cBP
+            split(nxt, True)
         for a in order:
             d = (rank - a) % NR
             kd = ts(r("WIN", MF + (d - 1) * 128, MF + d * 128), r("WIN", GB + (d - 1) * 384, GB + d * 384, 3), MAGIC, ALU.add, -MAGIC, ALU.add)
-        if last:
-            dma("y", hb(T.ys[:, :]), r("UB", 0, 2048), "oy", after=[kd])
 
         def ch(nm, c, base=0):
             return r(nm, base + c * 512, base + (c + 1) * 512)
@@ -524,17 +521,24 @@ def rank_program(g, core, T, topo):
         vote(2); bym(3); evac(2); scat(1); vote(3); evac(3); scat(2); scat(3)
 
         for i in range(8):
-            dma("y", r("H", HG, HG + 896, p=slice(i, 128, 16)), r("XS", i * NP + E, (i + 1) * NP, p=slice(i, 128, 16)), "dg")
+            dma("y", r("H", 0, NP, p=slice(i, 128, 16)), r("XS", i * NP, (i + 1) * NP, p=slice(i, 128, 16)), "dg")
         for i in range(8):
-            for nm in ("H", "H2"):
-                dma("y", r(nm, 0, E, p=slice(i, 128, 16)), r("XS", i * NP, i * NP + E, p=slice(i, 128, 16)), "do")
+            dma("y", r("H2", 0, E, p=slice(i, 128, 16)), r("XS", i * NP, i * NP + E, p=slice(i, 128, 16)), "do")
 
         def back(q, es):
             d = (rank - q) % NR
-            return (cores[q], r("H", HG + (d - 1) * 128, HG + d * 128), r("RET", (d - 1) * 128, d * 128), "ret", es)
+            return (cores[q], r("H", E + (d - 1) * 128, E + d * 128), r("RET", (d - 1) * 128, d * 128), "ret", es)
         fo = sorted(far, key=lambda q: (q - rank) % NR)
         send([back(q, offe[j * q2:(j + 1) * q2]) for j, q in enumerate(fo[:4])] + [back(q, one) for q in mate], "rsent", after=fw)
-        send([back(q, offe[j * h4:(j + 1) * h4]) for j, q in enumerate(fo[4:])], "rsent")
+        ks = send([back(q, offe[j * h4:(j + 1) * h4]) for j, q in enumerate(fo[4:])], "rsent")
+        ts(bl(5), hl(1), 16.0, ALU.is_equal, wt, ALU.mult)
+        if rnd == 0:
+            constants_b()
+        if last:
+            act(r("PM"), r("WIN", MO, MO + 2048), AF.Copy, scale=-4064.0 / 4096.0)
+            tt(r("UB", 0, 2048, 2), r("WIN", 1, 2048, 2), r("PM", 1, 2048, 2), ALU.add)
+            tt(r("UB", 1, 2048, 2), r("WIN", 0, 2048, 2), r("PM", 0, 2048, 2), ALU.add)
+            dma("y", hb(T.ys[:, :]), r("UB", 0, 2048), "oy", after=[ks])
         tot = len(one)
         for a in far:
             fa = sorted([x for x in range(NR) if topo.chip(cores[x]) != topo.chip(cores[a])], key=lambda x: (x - a) % NR)
@@ -542,15 +546,15 @@ def rank_program(g, core, T, topo):
         arrive("ret", tot, r("RET"))
         if not last:
             expand(bl(0), bl(1), "WP", PMB)
-            lists(cBP)
-            ts(of(oT2), w(cBP), 2048.0, ALU.min)
-            tt(w(cDB), w(cBP), w(cB), ALU.subtract)
+            lists(nxt)
+            ts(of(oT2), w(nxt), 2048.0, ALU.min)
+            tt(w(cDB), w(nxt), w(cB), ALU.subtract)
             for h in range(2):
                 tc(r("NB", h * 1024, (h + 1) * 1024), ind(r("WP"), of(oBX, h * 64, h * 64 + 64)), "s")
                 ext("NB", h * 1024, 64, r("PB" if h == 0 else "PY", 0, 64))
             act(w(cB0), hl(0), AF.Copy, bias=-2032.0)
             act(w(cB0 + 1), hl(1), AF.Copy, bias=-16.0)
-        tt(r("TT", 0, E), ind(r("H", 0, HG), of(oPT)), r("H2"), ALU.add)
+        tt(r("TT", 0, E), ind(r("H2"), of(oPT)), r("H", 0, E), ALU.add)
         tc(r("RV", 0, 128), ind(r("TT"), r("OP", 0, 8)))
         if not last:
             for h in range(2):

from concourse.bass import DstId, RemoteDMATransfer
from concourse.mybir import AluOpType as ALU, ActivationFunctionType as AF

E, NP, NR, HG = 2048, 2944, 8, 2064
GB, MO, MF, AO, WE = 2048, 4736, 6784, 7680, 9728
MAGIC = 1.5 * 2.0 ** 35
F, B, I, U = "float32", "bfloat16", "int32", "uint16"
SCRATCH = {
    "WIN": ("sbuf", [128, WE], F), "X0": ("sbuf", [128, 2064], F), "UA": ("sbuf", [128, 2064], F),
    "UB": ("sbuf", [128, 2064], F), "MH": ("sbuf", [128, 2048], F), "A1": ("sbuf", [128, 2048], F),
    "X1": ("sbuf", [128, 2048], F), "H2": ("sbuf", [128, HG], B), "XS": ("sbuf", [128, 8 * NP], B), "H": ("sbuf", [128, HG + 896], B), "TT": ("sbuf", [128, 2064], B),
    "WN": ("sbuf", [128, 2176], B), "WP": ("sbuf", [128, 2176], B), "NA": ("sbuf", [128, 2064], B), "NB": ("sbuf", [128, 2064], B),
    "EX": ("sbuf", [128, 2048], B), "XH": ("sbuf", [128, 2048], B), "XL": ("sbuf", [128, 2048], B),
    "CV": ("sbuf", [128, 1024], B), "CD": ("sbuf", [128, 1024], I), "CI": ("sbuf", [128, 128], I), "SI": ("sbuf", [128, 8], I),
    "OF": ("sbuf", [128, 16 * 128], U), "OP": ("sbuf", [128, 64], U),
    "W": ("sbuf", [128, 32 * 128], F), "WI": ("sbuf", [128, 5 * 128], I), "HL": ("sbuf", [128, 256], B), "BL": ("sbuf", [128, 768], B),
    "K": ("sbuf", [128, 5 * 128], F), "KB": ("sbuf", [128, 8 * 128], B), "PC": ("sbuf", [128, 8], F), "PI": ("sbuf", [128, 8], I),
    "PG": ("sbuf", [128, 512], F), "PAY": ("sbuf", [128, 384], F), "PF": ("sbuf", [128, 384], F), "SG": ("sbuf", [128, 768], B),
    "RET": ("sbuf", [128, 896], B), "RV": ("sbuf", [128, 512], B), "SM": ("sbuf", [128, 64], F),
    "PM": ("psum", [128, 2048], F), "PA": ("psum", [128, 512], F), "PB": ("psum", [128, 512], F),
    "PX": ("psum", [128, 512], F), "PY": ("psum", [128, 512], F),
}
SEMAPHORES = ["cv", "cs", "ct", "cg", "ld0", "ld1", "ld2", "ld3", "ld4", "xz", "tw0", "tw1", "tw2", "tw3", "dg", "do", "oy", "oc", "sent", "fwd", "rsent", "ret"] + \
             ["ga%d" % d for d in range(1, 8)]


def rank_program(g, core, T, topo):
    rank = T.rank_of(core)
    if rank is None:
        return
    cores = list(T.cores)
    Q = {"v": g.vector, "s": g.scalar, "t": g.tensor, "g": g, "y": g.sync}
    ops, acc, cnt = [], {}, {}

    def r(name, lo=None, hi=None, step=None, p=None):
        w = SCRATCH[name][1][1]
        lo = 0 if lo is None else lo
        hi = w if hi is None else hi
        ps = slice(None) if p is None else p
        ap = T[name][ps, lo:hi] if step is None else T[name][ps, lo:hi:step]
        return {"ap": ap, "rg": [(name, lo, hi)], "off": []}

    def ind(win, off):
        return {"ap": win["ap"].indirect(off["ap"]), "rg": win["rg"], "off": off["rg"]}

    def add(q, fn, wr, rd, kind="c", sem=None, inc=0, after=()):
        k = len(ops)
        W_ = [x for a in wr for x in a["rg"]]
        R_ = [x for a in rd for x in a["rg"]] + [x for a in list(wr) + list(rd) for x in a["off"]]
        deps = set(after)
        for rg, isw in [(x, True) for x in W_] + [(x, False) for x in R_]:
            ps = SCRATCH[rg[0]][0] == "psum"
            for (j, lo, hi, jw) in acc.get(rg[0], []):
                o = ops[j]
                if ps and o["q"] != q:
                    if lo // 512 <= (rg[2] - 1) // 512 and rg[1] // 512 <= (hi - 1) // 512:
                        deps.add(j)
                    continue
                if hi <= rg[1] or rg[2] <= lo or not (jw or isw) or (q == "t" and o["q"] == "t"):
                    continue
                if not (kind == "d" and o["kind"] == "d" and o["sem"] == sem):
                    deps.add(j)
        for rg, isw in [(x, True) for x in W_] + [(x, False) for x in R_]:
            acc.setdefault(rg[0], []).append((k, rg[1], rg[2], isw))
        waits = {}
        for j in deps:
            o = ops[j]
            if o["kind"] != "c":
                waits[o["sem"]] = cnt[o["sem"]]
        if sem is not None:
            cnt[sem] = cnt.get(sem, 0) + inc
        ops.append({"q": q, "fn": fn, "kind": kind, "sem": sem, "deps": sorted(deps), "waits": waits, "tot": cnt.get(sem, 0)})
        return k

    def tc(out, a, q="v"):
        if q == "s":
            return act(out, a, AF.Identity)
        return add("v", lambda: g.vector.tensor_copy(out["ap"], a["ap"]), [out], [a])

    def tt(out, a, b, op):
        return add("v", lambda: g.vector.tensor_tensor(out["ap"], a["ap"], b["ap"], op), [out], [a, b])

    def ts(out, a, s1, op0, s2=None, op1=None):
        rd = [a] + [x for x in (s1, s2) if isinstance(x, dict)]
        v1 = s1["ap"] if isinstance(s1, dict) else s1
        v2 = s2["ap"] if isinstance(s2, dict) else s2
        if op1 is None:
            return add("v", lambda: g.vector.tensor_scalar(out["ap"], a["ap"], v1, None, op0), [out], rd)
        return add("v", lambda: g.vector.tensor_scalar(out["ap"], a["ap"], v1, v2, op0, op1), [out], rd)

    def ms(out, c):
        return add("v", lambda: g.vector.memset(out["ap"], c), [out], [])

    def act(out, a, f, scale=1.0, bias=0.0):
        rd = [a] + ([bias] if isinstance(bias, dict) else [])
        bv = bias["ap"] if isinstance(bias, dict) else bias
        return add("s", lambda: g.scalar.activation(out["ap"], a["ap"], f, bias=bv, scale=scale), [out], rd)

    def mm(out, l, x, start, stop):
        return add("t", lambda: g.tensor.matmul(out["ap"], l["ap"], x["ap"], start, stop), [out], [l, x])

    def mms(out, pairs):
        for k, (l, x) in enumerate(pairs):
            mm(out, l, x, k == 0, k == len(pairs) - 1)

    def iota(out, pat, base, ch):
        return add("g", lambda: g.iota(out["ap"], pat, base, ch, allow_small_or_imprecise_dtypes=True), [out], [])

    def hb(ap):
        return {"ap": ap, "rg": [], "off": []}

    def dma(q, out, a, sem, after=()):
        return add(q, lambda: Q[q].dma_start(out["ap"], a["ap"]).then_inc(T.sem[sem], 16), [out], [a], "d", sem, 16, after)

    def arrive(sem, n, region):
        return add("x", None, [region], [], "x", sem, n)

    def send(items, lsem, after=()):
        trs = []
        for (dc, src, dst, rs, es) in items:
            rid, pid, _ = topo.addr(dc)
            trs.append(RemoteDMATransfer(dst_ids=[DstId(rid=rid, pnc=pid)], dma_engine_mask=sum(1 << e for e in es),
                                         remote_sem=T.sem[rs], src=src["ap"], dst=dst["ap"]))
        n = sum(len(it[4]) for it in items)
        return add("g", lambda: g.remote_dma_fused(trs, local_sem=T.sem[lsem]), [], [it[1] for it in items], "d", lsem, n, after)

    def w(k, n=1):
        return r("W", k * 128, (k + n) * 128)

    def wh(k, h):
        return r("W", k * 128 + h * 64, k * 128 + h * 64 + 64)

    def wi(k):
        return r("WI", k * 128, (k + 1) * 128)

    def of(k, lo=0, hi=128):
        return r("OF", k * 128 + lo, k * 128 + hi)

    def kf(k):
        return r("K", k * 128, (k + 1) * 128)

    def kb(k):
        return r("KB", k * 128, (k + 1) * 128)

    def bl(k):
        return r("BL", k * 128, (k + 1) * 128)

    def hl(h):
        return r("HL", h * 128, (h + 1) * 128)

    def ext(src, c0, n, out, more=()):
        mms(out, list(more) + [(r("EX", i * 128, (i + 1) * 128), r(src, c0 + i, c0 + 16 * n, 16)) for i in range(16)])

    def expand(hi, lo, win, banks):
        for k in range(4):
            nm, c0 = banks[k]
            for i in range(4 * k, 4 * k + 4):
                mms(r(nm, c0 + (i % 4) * 128, c0 + (i % 4 + 1) * 128),
                    [(r("XH", i * 128, (i + 1) * 128), hi), (r("XL", i * 128, (i + 1) * 128), lo)])
        for k in range(4):
            tc(r(win, k * 512, (k + 1) * 512), r(banks[k][0], banks[k][1], banks[k][1] + 512), "s")

    PMB = [("PM", k * 512) for k in range(4)]
    ALT = [("PM", 1536), ("PA", 0), ("PB", 0), ("PY", 0)]
    (cB, cR1, cR2, cBP, cUH, cIO, cEC, cD, cP0, cPU, cDB, t0, t1, t2, t3, t4, t5, t6, t7, cBX, cDX) = range(21)
    cDD, cE1, cE2, cB0, cDL = 22, 24, 26, 28, 30
    oN = [0, 2, 3, 4, 5, 6]
    o1, oBX, oT2, oBU, oBM, oH, oR, oX, oPT = 1, 7, 8, 9, 10, 11, 12, 13, 14

    mate = [q for q in range(NR) if q != rank and topo.chip(cores[q]) == topo.chip(core)]
    far = [q for q in range(NR) if topo.chip(cores[q]) != topo.chip(core)]

    def gate(a, q):
        on = [x for x in range(NR) if topo.chip(cores[x]) == topo.chip(cores[q])]
        same = [x for x in on if topo.die(cores[x]) == topo.die(cores[a])]
        return (same or on)[0]

    def near(q):
        return topo.mates(topo.chip(core), topo.chip(cores[q]))

    def planar(q):
        return topo.same_plane(topo.chip(core), topo.chip(cores[q]))
    both = [q for q in far if near(q)]
    direct = sorted([q for q in far if gate(rank, q) == q and not near(q)], key=planar)
    relay = sorted([a for a in far if gate(a, rank) == rank and not near(a)], key=planar)
    offe = topo.engines(core, cores[far[0]])
    one = [e for e in topo.engines(core, cores[mate[0]]) if e not in offe]
    h4, q2 = len(offe) // 2, len(offe) // 4

    def gslot(d):
        return r("WIN", GB + (d - 1) * 384, GB + d * 384)

    dma("y", r("CI"), hb(T.cur0[:, :]), "ld0")
    dma("y", r("CD", 0, 512), hb(T.cand[:, 0:512]), "ld1")
    dma("s", r("CD", 512, 1024), hb(T.cand[:, 512:1024]), "ld2")
    dma("s", r("CV"), hb(T.cov[:, :]), "ld3")
    dma("y", r("SI"), hb(T.shown[:, :]), "ld4")
    add("g", lambda: g.iota(T.PI[:, 0:1], [[0, 1]], 0, 1), [r("PI", 0, 1)], [])
    iota(kf(0), [[2, 8], [-1, 2], [16, 8]], 1, 0)
    iota(w(cIO), [[16, 128]], 0, 1)
    iota(kf(2), [[1, 128]], 0, 0)
    iota(kf(1), [[2, 64], [-1, 2]], 1, 0)
    iota(r("NA", 0, 2048), [[-8, 16], [1, 8], [8, 16]], 0, 0)
    iota(kf(3), [[1, 8], [0, 16]], 0, 0)
    ms(r("XH"), 0.0)
    act(r("H", 0, 2048), r("XH"), AF.Copy)
    act(r("H", 2048, HG + 896), r("XH", 0, HG + 896 - 2048), AF.Copy)
    ms(r("XL"), 0.0)
    for i in range(8):
        dma("y", r("XS", i * NP, (i + 1) * NP, p=slice(i, 128, 16)), r("H", 0, NP, p=slice(i, 128, 16)), "xz")
    dma("y", r("H2"), r("H", 0, HG), "xz")
    pc = [r("PC", k, k + 1) for k in range(8)]

    def mask(t):
        ts(r("PM", t * 128, (t + 1) * 128), r("CI"), float((t - 2) % 8), ALU.is_equal)

    def names(k, dst):
        c0 = (2 - k) * 128
        tt(r("A1", 0, 512), r("CD", 0, 512), r("PM", c0, c0 + 512), ALU.mult)
        tt(r("PX"), r("CD", 512, 1024), r("PM", c0 + 512, c0 + 1024), ALU.mult)
        tt(r("A1", 1024, 1536), r("A1", 0, 512), r("PX"), ALU.add)
        tt(r("A1", 1536, 1792), r("A1", 1024, 1280), r("A1", 1280, 1536), ALU.add)
        tt(w(dst), r("A1", 1536, 1664), r("A1", 1664, 1792), ALU.add)

    def split(src, half):
        tc(wi(0), w(src))
        ts(wi(1), wi(0), 15, ALU.bitwise_and)
        ts(wi(2), wi(0), 1, ALU.bitwise_and)
        tt(bl(0), w(src), wi(1), ALU.subtract)
        if half:
            tt(bl(1), w(cUH), wi(1), ALU.add)
        tc(bl(2), wi(1))

    def lists(src):
        ts(bl(3), wi(2), -256.0, ALU.mult, 128.0, ALU.add)
        ts(bl(4), w(src), 2048.0, ALU.is_ge, 4096.0, ALU.mult)
        mms(r("PX", 256, 384), [(kb(6), bl(0)), (kb(7), bl(2)), (kb(5), bl(3)), (kb(5), bl(4))])
        tt(w(t6), w(src), w(cIO), ALU.is_equal)
        act(w(t7), w(t6), AF.Copy, scale=8192.0)
        act(w(cDD), bl(0), AF.Copy, bias=-2032.0)
        act(w(cDD + 1), bl(2), AF.Copy, bias=-16.0)
        ts(of(oBX), r("PX", 256, 384), 2175.0, ALU.min)
        if src == cB:
            tc(w(cBX), r("PX", 256, 384))
        else:
            tt(w(cDX), w(cBX), r("PX", 256, 384), ALU.subtract)
        tt(w(cEC), w(t7), w(cIO), ALU.add)

    for t in range(2, 10):
        mask(t)
    tc(pc[0], r("PI", 0, 1))
    ts(r("PI", 1, 2), r("PI", 0, 1), 4, ALU.arith_shift_right)
    ts(r("XH", 0, 2048, 16), kf(0), pc[0], ALU.is_equal)
    ts(r("XL", 1, 2048, 16), kf(0), pc[0], ALU.is_equal)
    tc(pc[1], r("PI", 1, 2))
    names(0, cB)
    split(cB, False)
    act(r("X0", 0, 2048, 2), r("CV"), AF.Copy, bias=4064.0)
    act(r("X0", 1, 2048, 2), r("CV"), AF.Copy, bias=4064.0)
    dma("y", r("X1"), r("X0", 0, 2048), "tw0")
    expand(bl(0), bl(2), "WP", ALT)
    ts(pc[2], pc[1], -16.0, ALU.mult)
    for k, s in ((5, 1.0), (6, 0.0625), (7, 128.0)):
        ts(kb(k), kf(2), pc[0], ALU.is_equal, s, ALU.mult)
    ts(w(cIO), w(cIO), pc[2], ALU.add)
    ms(r("WP", 2048, 2176), 128.0)
    ts(r("EX"), r("NA", 0, 2048), pc[1], ALU.is_equal)
    lists(cB)
    for h, q in ((0, "v"), (1, "s"), (2, "v"), (3, "s")):
        tc(r("NB", h * 512, (h + 1) * 512), ind(r("WP"), of(oBX, h * 32, (h + 1) * 32)), q)
        if h % 2:
            ext("NB", (h // 2) * 1024, 64, r("PB" if h == 1 else "PY", 0, 64))
    for k, s in enumerate((1.0, 0.0625, 128.0)):
        ts(kb(k), kf(1), pc[0], ALU.is_equal, s, ALU.mult)
    ms(r("X0", 2048, 2064), 0.0)
    ms(r("WN", 2048, 2176), 128.0)
    mask(0)
    mask(1)
    for h in range(2):
        tt(wh(cP0, h), r("PB" if h == 0 else "PY", 0, 64), wh(cEC, h), ALU.is_equal)
    tt(r("PA", 0, 128), w(cP0), w(cDD), ALU.mult)
    tt(r("PA", 128, 256), w(cP0), w(cDD + 1), ALU.mult)
    ts(hl(0), r("PA", 0, 128), 2032.0, ALU.add)
    ts(hl(1), r("PA", 128, 256), 16.0, ALU.add)
    sm = [r("SM", k * 8, k * 8 + 8) for k in range(8)]

    def constants_a():
        si = r("SI")
        pi = [r("WI", 384 + k * 8, 392 + k * 8) for k in range(4)]
        for nm in ("UA", "UB"):
            ms(r(nm, 2048, 2064), 0.0)
        for nm in ("NA", "NB"):
            ms(r(nm, 2048, 2064), 128.0)
        ts(pi[1], si, 14, ALU.bitwise_and)
        ts(pi[2], si, 1, ALU.bitwise_and)
        ts(pi[0], si, 4, ALU.arith_shift_right)
        ts(sm[0], pi[1], 128.0, ALU.mult, 128.0, ALU.add)
        ts(sm[1], pi[2], -128.0, ALU.mult)
        tc(r("OP", 0, 8), si)
        tt(sm[0], sm[0], pi[0], ALU.add)
        ts(sm[4], si, -2048.0, ALU.add)
        ts(pc[3], pc[0], 96.0, ALU.add)
        tt(sm[0], sm[0], sm[1], ALU.add)
        ts(pc[4], pc[3], 128.0, ALU.is_ge, -128.0, ALU.mult)
        tc(r("OP", 32, 40), sm[0])
        tt(pc[3], pc[3], pc[4], ALU.add)
        ts(kf(0), kf(2), pc[0], ALU.is_equal)
        ts(kf(4), kf(2), pc[3], ALU.is_equal)

    def constants_b():
        ts(pc[5], pc[1], 6.0, ALU.is_ge, -8.0, ALU.mult)
        ts(pc[6], pc[1], 2.0, ALU.add)
        ms(r("TT", 2048, 2064), 0.0)
        tt(pc[6], pc[6], pc[5], ALU.add)
        tt(w(cR2), w(cR2), w(cR1), ALU.subtract)
        ts(kb(4), kf(3), pc[6], ALU.is_equal)

    def slots():
        ts(w(t3), r("CI"), float(NP), ALU.mult)
        tc(of(oBM), w(cB))
        tt(w(t3), w(t3), w(cB), ALU.add)
        act(w(t4), w(cB), AF.Copy, scale=3.0, bias=-4096.0)
        ts(w(t5), w(cB), 2047.5, ALU.is_lt, float(AO - 1), ALU.mult)
        tc(of(oX), w(t3))

    for rnd in range(3):
        last = rnd == 2
        wt = 2.0 ** (24 * rnd)
        mms(r("PX", 0, 128), [(kb(0), hl(0)), (kb(0), hl(1))])
        mms(r("PX", 128, 256), [(kb(1), hl(0)), (kb(2), hl(1))])
        tc(r("OF", 0, 256), r("PX", 0, 256))
        expand(hl(0), hl(1), "WN", ALT if rnd == 0 else PMB)
        ub = ["X0", "UA", "UB", "UA", "UB", "UA", "WIN"]
        nb = ["WN", "NA", "NB", "NA", "NB", "NA"]

        def twin(t, c):
            o, a = r("MH", c * 512, (c + 1) * 512), r(ub[t], c * 512, (c + 1) * 512)
            if c % 2 == t % 2:
                dma("y", o, a, "tw%d" % c)
            else:
                add("g", lambda: g.affine_select(o["ap"], a["ap"], [[0, 512]], ALU.is_ge, 0.0, 0, 0), [o], [a])

        def ustep(t, lo, hi):
            cs = list(range(lo // 512, hi // 512))
            if t % 2:
                cs = [c ^ 1 for c in cs]
            for c in cs:
                tt(r(ub[t], c * 512, (c + 1) * 512), ind(r(ub[t - 1], 0, 2064), of(oN[t - 1], c * 32, c * 32 + 32)),
                   r("X1" if t == 1 else "MH", c * 512, (c + 1) * 512), ALU.add)
                if t < 6:
                    twin(t, c)

        def nstep(k, h):
            tc(r(nb[k], h * 1024, (h + 1) * 1024), ind(r(nb[k - 1]), of(o1 if k == 1 else oN[k - 1], h * 64, h * 64 + 64)), "s")
            if (k, h) != (5, 1):
                ext(nb[k], h * 1024, 64, r("PX" if h == 0 else "PY", 0, 64))
            if rnd == 0 and k in (2, 3):
                for i in range(4 * h, 4 * h + 4):
                    c0 = (k - 2) * 1024 + i * 128
                    mm(r("PB", (k - 2) * 128, (k - 1) * 128), kf(0), r("A1", c0, c0 + 128), i == 0, i == 7)
            if rnd == 0 and (k, h) == (5, 0):
                tc(w(cR1, 2), r("PB", 0, 256), "s")

        def conv(k, h):
            tc(of(oN[k], h * 64, h * 64 + 64), r("PX" if h == 0 else "PY", 0, 64))

        def small(j, win, lo, n):
            tc(r("SG", j * 256, j * 256 + 16 * n), ind(r(win), r("OP", lo, lo + n)), "s")
            ext("SG", j * 256, n, r("PA", j * 16, j * 16 + n))

        ustep(1, 0, 2048)
        if rnd == 0:
            constants_a()
            for k in (1, 2):
                tt(r("A1", (k - 1) * 1024, k * 1024), r("CD"), r("PM", (2 - k) * 128, (2 - k) * 128 + 1024), ALU.mult)
        else:
            mv = r("PB", 0, 128)
            tt(w(t0), w(cDB), mv, ALU.mult)
            tt(w(t2), w(cDX), mv, ALU.mult)
            tt(wi(4), r("CI"), mv, ALU.add)
            if rnd == 1:
                tt(w(t1), w(cR2), mv, ALU.mult)
            tt(w(cB), w(cB), w(t0), ALU.add)
            tt(w(cBX), w(cBX), w(t2), ALU.subtract)
            ts(r("CI"), wi(4), 7, ALU.bitwise_and)
            ts(of(oBX), w(cBX), 2175.0, ALU.min)
            if rnd == 1:
                tt(w(cBP), w(t1), w(cR1), ALU.add)
        nstep(1, 0)
        nstep(1, 1)
        for k in range(1, 5):
            conv(k, 0)
            if k == 4:
                small(1, "NB", 0, 16)
            nstep(k + 1, 0)
            ustep(k + 1, 0, 1024)
            conv(k, 1)
            if k == 1:
                small(0, "WN", 32, 8)
            if k == 4:
                tc(r("OP", 48, 64), r("PA", 16, 32))
                small(2, "NB", 48, 16)
            nstep(k + 1, 1)
            ustep(k + 1, 1024, 2048)
            if k == 1:
                ts(sm[3], r("PA", 0, 8), 2047.5, ALU.is_ge)
                tc(r("OP", 8, 16), r("PA", 0, 8))
                tt(sm[3], sm[3], sm[4], ALU.mult)
            if k == 2:
                tt(sm[3], sm[3], r("PA", 0, 8), ALU.add)
            if k == 3:
                tc(r("OP", 40, 48), sm[3])
        tc(r("OP", 16, 32), r("PA", 32, 48))
        tc(r("PG", 0, 256), ind(r("UA"), r("OP", 0, 16)))
        conv(5, 0)
        tt(r("PG", 256, 512), ind(r("UA"), r("OP", 16, 32)), r("PG", 0, 256), ALU.add)
        mm(r("PB", 0, 256), kf(4), r("PG", 256, 512), True, True)
        ext("NA", 1024, 64, r("PY", 0, 64))
        tc(r("NB", 0, 2048), ind(r("WN"), of(oBX)), "s")
        ustep(6, 0, 512)
        ts(r("PF", 0, 256), r("PB", 0, 256), MAGIC, ALU.add, -MAGIC, ALU.add)
        tc(r("PAY", 0, 384, 3), r("PB", 0, 128))
        tt(r("PF", 256, 384), r("PF", 128, 256), r("PB", 0, 128), ALU.mult)
        tt(r("PA", 128, 256), r("PF", 0, 128), r("PB", 128, 256), ALU.mult)
        tc(r("PAY", 2, 384, 3), r("PF", 128, 256))
        tt(r("PAY", 1, 384, 3), r("PF", 256, 384), r("PA", 128, 256), ALU.subtract)

        def out(q, es):
            d = (q - rank) % NR
            return (cores[q], r("PAY"), gslot(d), "ga%d" % d, es)
        for j, q in enumerate(direct):
            send([out(q, offe)] + [out(x, one) for x in mate if j == 0], "sent")
        send([out(q, offe[j * h4:(j + 1) * h4]) for j, q in enumerate(both)], "sent")
        order = mate + relay + both + [a for a in far if a not in relay + both]
        for a in order:
            d = (rank - a) % NR
            arrive("ga%d" % d, h4 if a in both else (len(offe) if a in relay else len(one)), gslot(d))
        fw = []
        for a in relay:
            d2 = (mate[0] - a) % NR
            fw.append(send([(cores[mate[0]], gslot((rank - a) % NR), gslot(d2), "ga%d" % d2, one)], "fwd"))
        conv(5, 1)
        ustep(6, 512, 2048)
        ext("NB", 0, 128, r("PX", 0, 128))
        mms(r("PX", 128, 256), [(kb(5), hl(0)), (kb(5), hl(1))])
        ts(r("WIN", MO + 1536, MO + 2048), r("WIN", 1536, 2048), MAGIC, ALU.add, -MAGIC, ALU.add)
        slots()
        for lo, hi in ((0, 1024), (1024, 1536)):
            act(r("MH", lo, hi), r("WIN", lo, hi), AF.Copy, bias=MAGIC)
            act(r("WIN", MO + lo, MO + hi), r("MH", lo, hi), AF.Copy, bias=-MAGIC)
            act(r("PM", lo, hi), r("MH", lo, hi), AF.Copy, bias=-MAGIC)
        tc(r("PM", 1536, 2048), r("WIN", MO + 1536, MO + 2048), "s")
        if rnd == 0:
            ts(kb(3), kf(3), pc[1], ALU.is_equal)
        tt(w(t4), w(t4), w(cB), ALU.max)
        tc(of(oPT), r("PX", 128, 256))
        tt(w(t5), w(t5), w(t4), ALU.add)
        tc(of(oBU), w(t4))
        ts(w(t0), w(t5), float(2 - MO), ALU.add)
        ts(of(oR), w(t5), float(1 - GB), ALU.add)
        tt(w(t0), w(t0), r("PX", 0, 128), ALU.min)
        ms(r("PC", 7, 8), -8.0 * wt)
        ts(of(oH), w(t0), float(MO - GB), ALU.add)
        if not last:
            ts(w(cUH), hl(1), 16.0, ALU.is_equal, 0.5, ALU.mult)
            nxt = cR1 if rnd == 0 else cBP
            split(nxt, True)
        for a in order:
            d = (rank - a) % NR
            kd = ts(r("WIN", MF + (d - 1) * 128, MF + d * 128), r("WIN", GB + (d - 1) * 384, GB + d * 384, 3), MAGIC, ALU.add, -MAGIC, ALU.add)

        def ch(nm, c, base=0):
            return r(nm, base + c * 512, base + (c + 1) * 512)

        def oc(k, c):
            return of(k, c * 32, c * 32 + 32)

        def alt(c):
            return r("PB" if c % 2 == 0 else "PY")

        def own(c):
            return r("PA" if c % 2 == 0 else "PX")

        def gub(c):
            act(ch("UA", c), ind(r("WIN", 0, MO), oc(oBU, c)), AF.Identity)

        def gmh(c):
            act(ch("MH", c), ind(r("WIN", GB, AO), oc(oH, c)), AF.Identity)

        def a1(c):
            tt(ch("A1", c), ind(r("WIN", MO, AO), oc(oBM, c)), ch("WIN", c), ALU.mult)

        def bym(c):
            tt(own(c), ch("UA", c), ch("PM", c), ALU.mult)

        def dif(c):
            tt(ch("WIN", c, AO), ch("A1", c), own(c), ALU.subtract)

        def sabs(c):
            act(alt(c), ch("WIN", c, AO), AF.Abs)

        def left(c):
            tt(ch("A1", c), ch("MH", c), alt(c), ALU.mult)

        def gg(c):
            act(ch("UA", c), ind(r("WIN", GB, WE), oc(oR, c)), AF.Abs)

        def vote(c):
            tt(ch("NA", c), ch("A1", c), own(c), ALU.is_lt)
            mm(alt(c), kb(3), ch("NA", c), True, True)

        def evac(c):
            act(ch("NB", c), alt(c), AF.Relu, scale=wt, bias=r("PC", 7, 8))

        def scat(c):
            tc(ind(r("XS"), oc(oX, c)), ch("NB", c))

        gub(0); gub(1); a1(0); bym(0); a1(1); dif(0); gmh(0); gub(2); bym(1); a1(2); dif(1); sabs(0); gub(3); left(0)
        gmh(1); sabs(1); bym(2); a1(3); dif(2); left(1); gmh(2); bym(3); gmh(3); sabs(2); dif(3); left(2)
        gg(0); sabs(3); bym(0); left(3); gg(1); bym(1); vote(0); gg(2); evac(0); vote(1); bym(2); gg(3); evac(1); scat(0)
        vote(2); bym(3); evac(2); scat(1); vote(3); evac(3); scat(2); scat(3)

        for i in range(8):
            dma("y", r("H", 0, NP, p=slice(i, 128, 16)), r("XS", i * NP, (i + 1) * NP, p=slice(i, 128, 16)), "dg")
        for i in range(8):
            dma("y", r("H2", 0, E, p=slice(i, 128, 16)), r("XS", i * NP, i * NP + E, p=slice(i, 128, 16)), "do")

        def back(q, es):
            d = (rank - q) % NR
            return (cores[q], r("H", E + (d - 1) * 128, E + d * 128), r("RET", (d - 1) * 128, d * 128), "ret", es)
        fo = sorted(far, key=lambda q: (q - rank) % NR)
        send([back(q, offe[j * q2:(j + 1) * q2]) for j, q in enumerate(fo[:4])] + [back(q, one) for q in mate], "rsent", after=fw)
        ks = send([back(q, offe[j * h4:(j + 1) * h4]) for j, q in enumerate(fo[4:])], "rsent")
        ts(bl(5), hl(1), 16.0, ALU.is_equal, wt, ALU.mult)
        if rnd == 0:
            constants_b()
        if last:
            act(r("PM"), r("WIN", MO, MO + 2048), AF.Copy, scale=-4064.0 / 4096.0)
            tt(r("UB", 0, 2048, 2), r("WIN", 1, 2048, 2), r("PM", 1, 2048, 2), ALU.add)
            tt(r("UB", 1, 2048, 2), r("WIN", 0, 2048, 2), r("PM", 0, 2048, 2), ALU.add)
            dma("y", hb(T.ys[:, :]), r("UB", 0, 2048), "oy", after=[ks])
        tot = len(one)
        for a in far:
            fa = sorted([x for x in range(NR) if topo.chip(cores[x]) != topo.chip(cores[a])], key=lambda x: (x - a) % NR)
            tot += q2 if fa.index(rank) < 4 else h4
        arrive("ret", tot, r("RET"))
        if not last:
            expand(bl(0), bl(1), "WP", PMB)
            lists(nxt)
            ts(of(oT2), w(nxt), 2048.0, ALU.min)
            tt(w(cDB), w(nxt), w(cB), ALU.subtract)
            for h in range(2):
                tc(r("NB", h * 1024, (h + 1) * 1024), ind(r("WP"), of(oBX, h * 64, h * 64 + 64)), "s")
                ext("NB", h * 1024, 64, r("PB" if h == 0 else "PY", 0, 64))
            act(w(cB0), hl(0), AF.Copy, bias=-2032.0)
            act(w(cB0 + 1), hl(1), AF.Copy, bias=-16.0)
        tt(r("TT", 0, E), ind(r("H2"), of(oPT)), r("H", 0, E), ALU.add)
        tc(r("RV", 0, 128), ind(r("TT"), r("OP", 0, 8)))
        if not last:
            for h in range(2):
                tt(wh(cD, h), r("PB" if h == 0 else "PY", 0, 64), wh(cEC, h), ALU.subtract)
            ts(r("PB", 128, 256), w(cD), 0.5, ALU.is_equal)
            ts(r("PB", 256, 384), w(cD), 0.0, ALU.is_equal)
            for h in range(2):
                tt(w(cE1 + h), w(cDD + h), r("PB", 128, 256), ALU.mult)
            for h in range(2):
                tt(w(cE2 + h), w(cDD + h), r("PB", 256, 384), ALU.mult)
            tt(w(cE1, 2), w(cE1, 2), w(cB0, 2), ALU.subtract)
        mms(r("PA", 0, 128), [(kb(4), r("RET", (d - 1) * 128, d * 128)) for d in range(1, NR)])
        tt(r("RV", 128, 256), r("RV", 0, 128), r("PA", 0, 128), ALU.add)
        tc(r("RV", 256, 384), r("PA", 0, 128), "s")
        tc(ind(r("TT"), r("OP", 0, 8)), r("RV", 128, 256))
        tt(r("RV", 384, 512), ind(r("TT"), r("OP", 40, 48)), r("RV", 256, 384), ALU.add)
        tc(ind(r("TT"), r("OP", 40, 48)), r("RV", 384, 512))
        ext("TT", 0, 128, r("PX", 0, 128), more=[(kb(5), bl(5))])
        mv = r("PB", 0, 128)
        if not last:
            for h, q in ((0, "v"), (1, "s"), (2, "v"), (3, "s")):
                tc(ch("NA", h), ind(r("TT"), oc(oT2, h)), q)
            for h in range(2):
                ext("NA", h * 1024, 64, r("PY", h * 64, h * 64 + 64))
        ts(mv, r("PX", 0, 128), 0.5 * wt, ALU.is_ge)
        if not last:
            for h in range(2):
                tt(r("PB", 128 + h * 128, 256 + h * 128), w(cE1 + h), mv, ALU.mult)
            for h in range(2):
                tt(w(cDL + h), w(cE2 + h), mv, ALU.mult)
            tt(w(cB0, 2), r("HL"), r("PB", 128, 384), ALU.add)
            ts(r("PA", 0, 128), r("PY", 0, 128), 0.5 * wt, ALU.is_ge)
            for h in range(2):
                tt(r("PA", 128 + h * 128, 256 + h * 128), w(cDL + h), r("PA", 0, 128), ALU.mult)
            tt(r("HL"), w(cB0, 2), r("PA", 128, 384), ALU.add)
        else:
            tt(wi(4), r("CI"), mv, ALU.add)
            ts(wi(0), wi(4), 7, ALU.bitwise_and)
            tc(w(t0), wi(0))
            dma("y", hb(T.yc[:, :]), w(t0), "oc")

    csem = {"v": "cv", "s": "cs", "t": "ct", "g": "cg"}
    pos, clock, need = {}, {}, set()
    seen = {q: {} for q in Q}
    plan = []
    for k, o in enumerate(ops):
        q = o["q"]
        if q == "x":
            clock[k] = {o["sem"]: o["tot"]}
            plan.append(None)
            continue
        kn = seen[q]
        ws = []
        for j in sorted(o["deps"], reverse=True):
            p = ops[j]
            if p["kind"] == "c":
                key, val = "#" + p["q"], j
            else:
                key, val = p["sem"], o["waits"][p["sem"]]
            if kn.get(key, -1) >= val:
                continue
            ws.append((key, val))
            kn[key] = val
            if p["kind"] == "c":
                need.add(j)
            for a, b in clock[j].items():
                if kn.get(a, -1) < b:
                    kn[a] = b
        clock[k] = dict(kn)
        plan.append(ws)
    num = {q: 0 for q in csem}
    for k, o in enumerate(ops):
        if k in need:
            num[o["q"]] += 1
            pos[k] = num[o["q"]]
    for k, o in enumerate(ops):
        if o["q"] == "x":
            continue
        for key, val in plan[k]:
            if key[0] == "#":
                Q[o["q"]].wait_ge(T.sem[csem[key[1]]], pos[val])
            else:
                Q[o["q"]].wait_ge(T.sem[key], val)
        ins = o["fn"]()
        if k in need:
            ins.then_inc(T.sem[csem[o["q"]]], 1)
    for s in sorted(cnt):
        if max(seen[q].get(s, 0) for q in Q) < cnt[s]:
            g.wait_ge(T.sem[s], cnt[s])
